import numpy as np, ml_dtypes
CORES = [51,54,179,182]
N = 4
BF = ml_dtypes.bfloat16
W, C, TS, S = 2048, 256, 5, 1
B = W // C
SHAPES = np.array([[0, 15, 1, 2, 3, 4, 5, 6, 7, 8, 9, 10, 11, 12, 13, 14], [0, 1, 2, 15, 3, 14, 4, 13, 5, 12, 6, 11, 7, 10, 8, 9], [14, 15, 0, 13, 1, 12, 2, 11, 3, 10, 4, 9, 5, 8, 6, 7],
                   [1, 14, 0, 15, 2, 3, 4, 5, 6, 7, 8, 9, 10, 11, 12, 13], [7, 8, 0, 15, 1, 14, 2, 13, 3, 12, 4, 11, 5, 10, 6, 9], [3, 11, 0, 8, 1, 9, 2, 10, 4, 12, 5, 13, 6, 14, 7, 15],
                   [0, 2, 1, 3, 4, 15, 5, 14, 6, 13, 7, 12, 8, 11, 9, 10]])
def place(a, b, n):
    return ((a * b >> 5) + 37 * a + 11 * b + (n & 63)) & (W - 1)
def mate(o):
    p = np.zeros_like(o); np.put_along_axis(p, o, o[..., np.array([0, 1, 3, 2, 5, 4, 7, 6, 9, 8, 11, 10, 13, 12, 15, 14])], -1)
    return np.ascontiguousarray(np.moveaxis(p, -1, -2))
def loose(p):
    m = p == np.arange(16).reshape(1, 1, 16, 1)
    return np.argmax(m, axis=2), 15 - np.argmax(m[:, :, ::-1], axis=2)
def look(x, l, p, fr, z, a):
    lf = np.take_along_axis(l, fr[:, :, None, :], 2); lp = np.take_along_axis(l, p, 2); n = a[:, :, None, None]
    xk = np.take_along_axis(x, place(l, lp, n).reshape(N, 8, 1, 16 * C), 3).reshape(N, 8, 16, 16, C)
    yk = np.take_along_axis(x, place(lf, l, n).reshape(N, 8, 1, 16 * C), 3).reshape(N, 8, 16, 16, C)
    dx = np.sum(np.abs(xk - z[:, :, :, None, :]), axis=2); dy = np.sum(np.abs(yk - z[:, :, :, None, :]), axis=2)
    return xk, yk, dx, dx - dy
def parts(rng):
    x = rng.integers(0, 64, (N, 8, 16, W)); l = rng.integers(0, 4096, (N, 8, 16, C)); z = rng.integers(0, 64, (N, 8, 16, C))
    p = mate(np.argsort(rng.random((N, 8, C, 16)), axis=-1)); t = rng.integers(60, 241, (N, 8, TS))
    return x, l, p, z, t
def pack(x, l, p, z, t):
    return {"xt": np.ascontiguousarray(x.reshape(N, 128, W)).astype(np.float32).astype(BF), "nm": np.ascontiguousarray(l.reshape(N, 128, C)).astype(np.int32),
            "pr": np.ascontiguousarray(p.reshape(N, 128, C)).astype(np.int32), "z0": np.ascontiguousarray(z.reshape(N, 128, C)).astype(np.float32).astype(BF),
            "th": np.ascontiguousarray(np.repeat(t, 16, axis=1)).astype(np.int32)}
def plant(rng, x, l, p, z, used, q, g, i, zz, v, w, odd, last):
    c = rng.integers(0, 4096, (512, 16)); pp = p[q, g, :, i]; bd = np.flatnonzero(pp != np.arange(16)); fr = int(np.flatnonzero(pp == np.arange(16))[0])
    hx = place(c[:, bd], c[:, pp[bd]], 0); hy = place(c[:, fr:fr + 1], c[:, bd], 0); h = np.concatenate([hx, hy], axis=1); k = np.sort(h, axis=1)
    fit = np.all(k[:, 1:] != k[:, :-1], axis=1) & ~np.any(used[h], axis=1); j = int(np.argmax(fit))
    assert fit[j], "no fitting names"
    ax = np.zeros((16, len(bd)), np.int64) + np.reshape(v, (-1, 1)); ax[15, :-1] = odd; ax[15, -1] = last
    xx = x[q, g]; xx[:, hx[j]] = ax; xx[:, hy[j]] = w
    l[q, g, :, i] = c[j]; z[q, g, :, i] = zz; used[h[j]] = True
def setup_inputs(rng):
    return pack(*parts(rng))
def setup_inputs_spread(rng):
    x, l, p, z, t = parts(rng)
    x = (rng.random((N, 8, 16, W)) * np.exp2(rng.integers(0, 7, (N, 8, 1, W)))).astype(np.int64); x = np.where(rng.random((N, 8, 1, W)) < 0.5, 63 - x, x)
    l = np.where(rng.random((N, 8, 1, C)) < 0.5, np.exp2(12 * rng.random((N, 8, 16, C))).astype(np.int64) - 1, l); l = np.minimum(l, 4095)
    z = np.where(rng.random((N, 8, 1, C)) < 0.7, np.minimum(np.exp2(6 * rng.random((N, 8, 16, C))).astype(np.int64) - 1, 63), z)
    t = np.where(rng.random((N, 8, TS)) < 0.4, rng.integers(-1008, 1009, (N, 8, TS)), rng.integers(0, 300, (N, 8, TS)))
    return pack(x, l, p, z, t)
def setup_inputs_ends(rng):
    x, l, p, z, t = parts(rng)
    x = 63 * np.where(rng.random((N, 8, 1, W)) < 0.75, rng.integers(0, 2, (N, 8, 1, W)), rng.integers(0, 2, (N, 8, 16, W)))
    l = np.where(rng.random((N, 8, 16, C)) < 0.75, 4095 * rng.integers(0, 2, (N, 8, 16, C)), l)
    z = 63 * np.where(rng.random((N, 8, 1, C)) < 0.6, rng.integers(0, 2, (N, 8, 1, C)), rng.integers(0, 2, (N, 8, 16, C)))
    sh = rng.integers(0, 6, (N, 8, C)); sh[:, :, np.array([0, C // 2, C - 1])] = 1
    sh[:, :, np.array([1, 2, C - 3])] = 6; sh[1::2, :, C // 2] = 6; p = mate(SHAPES[sh])
    t = 2016 * rng.integers(0, 2, (N, 8, TS)) - 1008; t[:, 0] = 1008; t[:, 1] = -1008
    t[:, 2] = rng.choice(np.array([1007, 0, -1007, 500]), (N, TS)); t[:, 5] = rng.choice(np.array([1007, 0, -1007, 500]), (N, TS))
    t[:, 2, 0] = 1007; t[:, 5, 0] = 1007; t[:, 7, 0] = 1007
    for q in range(N):
        for g in range(8):
            used = np.zeros(W, bool); m = int(rng.integers(9, 16))
            plant(rng, x, l, p, z, used, q, g, C - 1, 63, 0, 63, 1, 0)
            plant(rng, x, l, p, z, used, q, g, C - 2, 0, 0, 63, 0, 0)
            plant(rng, x, l, p, z, used, q, g, 0, 63, 63, 0, 62, 63)
            plant(rng, x, l, p, z, used, q, g, C // 2, 63, 0, 63, 0, 0)
            plant(rng, x, l, p, z, used, q, g, 1, 63, 0, 0, 0, 1)
            plant(rng, x, l, p, z, used, q, g, C - 3, 63, 63, 0, 63, 62)
            plant(rng, x, l, p, z, used, q, g, 2, 63, np.where(np.arange(16) < m, 0, 63), 0, 62, 63)
    return pack(x, l, p, z, t)
def setup_inputs_corners(rng):
    x, l, p, z, t = parts(rng); p = mate(SHAPES[rng.integers(0, 6, (N, 8, C))])
    l[:, 0] = rng.integers(0, 4096, (N, 1, C)); t[:, 0] = rng.integers(-1, 1, (N, TS))
    for q in range(N): l[q, 1] = (0, 4095, 1, 2048, 4094, 77, 1023, 64)[(q + int(rng.integers(0, 8))) % 8]
    l[:, 2] = 4095 * rng.integers(0, 2, (N, 16, C))
    x[:, 3] = rng.integers(0, 64, (N, 16, 1)); t[:, 3] = rng.integers(-1, 1, (N, TS))
    z[:, 4] = 63 * rng.integers(0, 2, (N, 1, C))
    t[:, 7] = 2016 * rng.integers(0, 2, (N, TS)) - 1008
    fr, e = loose(p); s = look(x, l, p, fr, z, np.zeros((N, 8), np.int64))[3]
    best = np.max(np.where(p != np.arange(16).reshape(1, 1, 16, 1), s, -1008), axis=2)
    t[:, 5, 0] = best[:, 5, 0]; t[:, 6, 0] = np.maximum(best[:, 6, C - 1] - 1, -1008)
    return pack(x, l, p, z, t)
def setup_inputs_crowd(rng):
    x, l, p, z, t = parts(rng); x = rng.integers(1, 63, (N, 8, 16, W)); z = rng.integers(1, 63, (N, 8, 16, C))
    l[:, 4] = rng.integers(0, 4096, (N, 1, 1)); l[:, 6] = rng.integers(0, 4096, (N, 1, 1))
    t[:] = 1008; t[:, 1, 0] = 1007; t[:, 5, 0] = 1007
    for g in (2, 3, 6, 7): t[:, g] = -1008
    for q in range(N):
        for g, i in ((1, C - 1), (5, 0)): plant(rng, x, l, p, z, np.zeros(W, bool), q, g, i, 63, 0, 63, 0, 0)
        for g, i in ((3, 0), (7, C - 1)): plant(rng, x, l, p, z, np.zeros(W, bool), q, g, i, 0, 0, 63, 0, 0)
    return pack(x, l, p, z, t)
def check_inputs(d):
    bad = []
    for k, lo, hi in (("xt", 0, 63), ("nm", 0, 4095), ("pr", 0, 15), ("z0", 0, 63), ("th", -1008, 1008)):
        v = np.asarray(d[k]).astype(np.float64)
        if not (np.min(v) >= lo and np.max(v) <= hi): bad.append("range of " + k)
        elif np.any(v != np.floor(v)): bad.append("whole numbers in " + k)
    p = np.clip(np.asarray(d["pr"]).astype(np.int64), 0, 15).reshape(N, 8, 16, C); row = np.arange(16).reshape(1, 1, 16, 1)
    if np.any(np.take_along_axis(p, p, 2) != row): bad.append("pairs in pr")
    if np.any(np.sum(p == row, axis=2) != 2): bad.append("two free rows in pr")
    t = np.asarray(d["th"]).reshape(N, 8, 16, TS)
    if np.any(t != t[:, :, :1]): bad.append("rows of a group alike in th")
    return bad
def reference(xt, nm, pr, z0, th):
    x = xt.astype(np.float32).astype(np.int64).reshape(N, 8, 16, W); l = nm.astype(np.int64).reshape(N, 8, 16, C); p = pr.astype(np.int64).reshape(N, 8, 16, C)
    z = z0.astype(np.float32).astype(np.int64).reshape(N, 8, 16, C); tt = th.astype(np.int64).reshape(N, 8, 16, TS)[:, :, 0]
    row = np.arange(16).reshape(1, 1, 16, 1); fr, e = loose(p); a = np.zeros((N, 8), np.int64); ct = np.zeros((TS, N, 8), np.int64)
    for t in range(TS):
        at = (np.arange(N) + S * t) % N; xa = x[at]
        xk, yk, dx, s = look(xa, l, p, fr, z, a[at]); bonded = p != row
        top = np.where(bonded, s, -9999); k1 = np.argmax(top, axis=2); k2 = np.argmin(np.where(bonded, dx, 9999), axis=2)
        esc = np.max(top, axis=2) <= tt[at][:, :, t:t + 1]
        k = np.where(esc, k2, k1); kk = k[:, :, None, :]; q = np.take_along_axis(p, kk, 2); es = esc[:, :, None, :]
        px = np.take_along_axis(xk, k[:, :, None, None, :], 3)[:, :, :, 0]; py = np.take_along_axis(yk, k[:, :, None, None, :], 3)[:, :, :, 0]
        z = np.where(es, np.abs(z - px), (z + py) >> 1)
        ff = fr[:, :, None, :]; m = np.where(es, e[:, :, None, :], kk)
        p = np.where(row == ff, m, np.where(row == m, ff, p)); p = np.where(row == q, q, p); p = np.where(es & (row == kk), kk, p)
        q = q[:, :, 0]; fr = np.where(esc, k, q); e = np.where(esc, q, e)
        col = (B * np.arange(C) + (np.sum(z, axis=2) & (B - 1)))[:, :, None, :]
        new = (np.take_along_axis(xa, col, 3) + z) >> 1
        np.put_along_axis(xa, np.ascontiguousarray(np.broadcast_to(col, (N, 8, 16, C))), new, 3); x[at] = xa
        ct[t, at] = np.sum(esc, axis=2); a = a + ct[t]
    return {"yx": x.reshape(N, 128, W).astype(np.float32).astype(BF), "ye": np.ascontiguousarray(np.repeat(np.moveaxis(ct, 0, -1), 16, axis=1)).astype(np.float32),
            "yp": p.reshape(N, 128, C).astype(np.float32), "yf": fr.astype(np.float32), "yz": z.reshape(N, 128, C).astype(np.float32).astype(BF)}

@@ -1,0 +1,520 @@
+from concourse.mybir import dt, AluOpType as A, AxisListType, ActivationFunctionType as F
+
+N, TS = 4, 5
+VSET = ((7,), ())
+LAG = 2
+ADV = (5, 6)
+SCRATCH = {
+    "X": ("sbuf", [128, 2112], "bfloat16"), "NM": ("sbuf", [128, 256], "int32"), "PR": ("sbuf", [128, 256], "int32"),
+    "TH": ("sbuf", [128, 5], "int32"), "LL": ("sbuf", [128, 4, 2, 128], "float32"), "NQH": ("sbuf", [128, 256], "float16"),
+    "PT": ("sbuf", [128, 256], "float16"), "FMG": ("sbuf", [128, 256], "bfloat16"),
+    "OO": ("sbuf", [128, 3, 2, 128], "float32"), "A1": ("sbuf", [128, 3, 2, 128], "float32"),
+    "B1": ("sbuf", [128, 3, 2, 128], "float32"), "SXY": ("sbuf", [128, 3, 2, 2, 128], "float32"),
+    "ONE": ("sbuf", [128, 128], "float32"), "If": ("sbuf", [128, 128], "float32"), "BOa": ("sbuf", [128, 128], "float32"),
+    "BO": ("sbuf", [128, 128], "float32"), "PX": ("sbuf", [128, 2, 64], "float32"), "PM": ("sbuf", [128, 4, 4, 2, 16], "float16"),
+    "II": ("sbuf", [128, 256], "bfloat16"), "nI": ("sbuf", [128, 128], "bfloat16"), "PN": ("sbuf", [128, 128], "bfloat16"),
+    "Ih": ("sbuf", [128, 128], "float16"), "BOb": ("sbuf", [128, 128], "bfloat16"), "BOh": ("sbuf", [128, 128], "float16"),
+    "SEL": ("sbuf", [128, 2048], "float16"), "RX": ("sbuf", [128, 16], "bfloat16"), "KD": ("sbuf", [128, 256], "bfloat16"),
+    "KDF": ("sbuf", [128, 256], "bfloat16"), "C2": ("sbuf", [128, 256], "bfloat16"), "OB": ("sbuf", [128, 128], "bfloat16"),
+    "O5": ("sbuf", [128, 128], "float16"), "THD": ("sbuf", [128, 640], "float16"), "D0": ("sbuf", [128, 256], "float32"),
+    "RLi": ("sbuf", [128, 24], "int32"), "RL": ("sbuf", [128, 24], "uint16"), "PI": ("sbuf", [128, 32], "int32"),
+    "RM": ("sbuf", [128, 2], "uint16"), "DJ": ("sbuf", [128, 128], "int32"), "DD": ("sbuf", [128, 128], "float32"),
+    "M8": ("sbuf", [128, 128], "bfloat16"), "M1": ("sbuf", [128, 128], "bfloat16"), "JI": ("sbuf", [128, 8], "int32"),
+    "JC": ("sbuf", [128, 8], "bfloat16"), "J8": ("sbuf", [128, 8], "bfloat16"), "KR": ("sbuf", [128, 384], "bfloat16"),
+    "CM": ("sbuf", [128, 128], "bfloat16"), "COL": ("sbuf", [128, 16], "float32"), "PI2": ("sbuf", [128, 16], "int32"),
+    "ZL": ("sbuf", [128, 1280], "bfloat16"), "ZN": ("sbuf", [128, 1280], "bfloat16"),
+    "HL": ("sbuf", [128, 10, 2, 128], "float16"), "HN": ("sbuf", [128, 10, 2, 128], "float16"),
+    "PK": ("sbuf", [128, 5120], "bfloat16"), "PS": ("sbuf", [128, 5120], "bfloat16"),
+    "RI": ("sbuf", [128, 1600], "int32"), "RS": ("sbuf", [128, 1600], "int32"),
+    "OFF": ("sbuf", [128, 512], "uint16"), "WW": ("sbuf", [128, 8192], "bfloat16"), "AY": ("sbuf", [128, 4096], "bfloat16"),
+    "XR": ("sbuf", [128, 4096], "bfloat16"), "SC": ("sbuf", [128, 512], "float32"), "SE": ("sbuf", [128, 16], "int32"),
+    "TM": ("sbuf", [128, 64], "float32"), "KQ": ("sbuf", [128, 16], "int32"), "GMx": ("sbuf", [128, 256], "bfloat16"),
+    "LS": ("sbuf", [128, 16], "uint16"), "LC": ("sbuf", [128, 16], "uint16"), "AW": ("sbuf", [128, 256], "bfloat16"),
+    "SZ": ("sbuf", [128, 256], "float32"), "HZ": ("sbuf", [128, 256], "int32"), "UI": ("sbuf", [128, 32], "int32"),
+    "SX2": ("sbuf", [128, 256], "float32"), "HX2": ("sbuf", [128, 256], "int32"), "ES": ("sbuf", [128, 320], "bfloat16"),
+    "M3": ("sbuf", [128, 48], "int32"), "DF": ("sbuf", [128, 96], "float32"),
+    "UO": ("sbuf", [128, 128], "float32"), "MaL": ("sbuf", [128, 128], "float32"), "R1": ("sbuf", [128, 128], "float32"),
+    "UR": ("sbuf", [128, 128], "float32"), "QI": ("sbuf", [128, 128], "int32"), "LPi": ("sbuf", [128, 256], "int32"),
+    "Pi": ("sbuf", [128, 256], "int32"), "PP": ("sbuf", [128, 256], "float32"), "QQ": ("sbuf", [128, 256], "int32"),
+    "HB": ("sbuf", [128, 256], "int32"), "HF": ("sbuf", [128, 256], "float16"),
+    "MSK": ("sbuf", [128, 512], "float16"), "PRD": ("sbuf", [128, 512], "float16"), "T1": ("sbuf", [128, 256], "float32"),
+    "AT": ("sbuf", [128, 8], "float32"), "NC": ("sbuf", [128, 8], "float32"), "AI": ("sbuf", [128, 8], "int32"),
+    "YE": ("sbuf", [128, 5], "float32"), "YP": ("sbuf", [128, 256], "float32"), "YF": ("sbuf", [128, 256], "float32"),
+    "FA": ("sbuf", [128, 32], "bfloat16"), "P2": ("sbuf", [128, 256], "float32"),
+    "SB": ("psum", [128, 2048], "float32"), "KP": ("psum", [128, 512], "float32"), "HR": ("psum", [128, 2, 128], "float32"),
+    "ST": ("psum", [128, 512], "float32"), "TL": ("psum", [128, 512], "float32"),
+}
+PSUM = ("SB", "KP", "ST", "TL", "HR")
+KINDS = ("z", "h", "p", "r")
+SEMAPHORES = ["v", "p", "s", "gq", "sent", "dm0", "dm1", "dm2", "dm3", "dx0", "out"] + \
+    ["a%s%d%d" % (k, t, h) for t in range(1, TS) for h in range(2) for k in KINDS] + ["l%d" % t for t in range(1, N)]
+
+
+def rank_program(g, core, T, topo):
+    rank = T.rank_of(core)
+    if rank is None:
+        return
+    sem = T.sem
+    Q = {"v": g.vector, "p": g.tensor, "s": g.scalar, "gq": g, "sy": g.sync}
+    cnt, know, hist = {}, {q: {} for q in Q}, {}
+
+    def acc(q, rd, wr):
+        need = []
+        for regs, w in ((rd, False), (wr, True)):
+            for (b, lo, hi) in regs:
+                for e in hist.get(b, ()):
+                    if e[1] < hi and lo < e[2] and (w or e[3]) and not (e[0] == q and (q == "p" or not e[3])):
+                        need.append(e)
+        for e in sorted(need, key=lambda e: -e[5]):
+            if know[q].get(e[4], 0) < e[5]:
+                Q[q].wait_ge(sem[e[4]], e[5])
+                for s, n in list(e[6].items()) + [(e[4], e[5])]:
+                    know[q][s] = max(know[q].get(s, 0), n)
+
+    def note(q, rd, wr, s, n, snap):
+        for regs, w in ((rd, False), (wr, True)):
+            for (b, lo, hi) in regs:
+                old = [e for e in hist.get(b, []) if not (lo <= e[1] and e[2] <= hi and (w or (e[0] == q and not e[3])))]
+                hist[b] = old + [(q, lo, hi, w, s, n, snap)]
+
+    def do(q, fn, rd, wr, s=None, inc=1):
+        acc(q, rd, wr)
+        s = s or q
+        cnt[s] = cnt.get(s, 0) + inc
+        fn(Q[q]).then_inc(sem[s], inc)
+        note(q, rd, wr, s, cnt[s], dict(know[q]))
+
+    def ps(b, lo, hi):
+        return (b, lo // 512, (hi + 511) // 512) if b in PSUM else (b, lo, hi)
+
+    def c(b, lo=0, hi=None, st=1):
+        hi = T[b].shape[1] if hi is None else hi
+        return (T[b][:, lo:hi:st], ps(b, lo, hi))
+
+    def ind(w, o):
+        return (w[0].indirect(o[0]), w[1], o[1])
+
+    def op(q, fn, out, *ins):
+        rs = [r for x in ins for r in x[1:]]
+        do(q, fn, [r for r in rs if r[0] not in PSUM], [out[1]] + [r for r in rs if r[0] in PSUM] + list(out[2:]))
+
+    def tt(out, a, b, o):
+        op("v", lambda e: e.tensor_tensor(out[0], a[0], b[0], o), out, a, b)
+
+    def ts(out, a, s1, s2, o0, o1=None):
+        x = [s for s in (s1, s2) if isinstance(s, tuple)]
+        f1, f2 = [s[0] if isinstance(s, tuple) else s for s in (s1, s2)]
+        if o1 is None:
+            op("v", lambda e: e.tensor_scalar(out[0], a[0], f1, None, o0), out, a, *x)
+        else:
+            op("v", lambda e: e.tensor_scalar(out[0], a[0], f1, f2, o0, o1), out, a, *x)
+
+    def cp(out, a):
+        op("v", lambda e: e.tensor_copy(out[0], a[0]), out, a)
+
+    def ms(out, k):
+        op("v", lambda e: e.memset(out[0], k), out)
+
+    def scan(out, d):
+        op("v", lambda e: e.tensor_tensor_scan(out[0], T.D0[:, :], d[0], 0.0, A.add, A.max), out, c("D0"), d)
+
+    def act(out, a, f, bias=0.0, scale=1.0):
+        x = [s for s in (bias,) if isinstance(s, tuple)]
+        bb = bias[0] if isinstance(bias, tuple) else bias
+        op("s", lambda e: e.activation(out[0], a[0], f, bias=bb, scale=scale), out, a, *x)
+
+    def mm(out, l, r, start, stop):
+        op("p", lambda e: e.matmul(out[0], l[0], r[0], start, stop), out, l, r)
+
+    def dma(q, out, in_, s, rd, wr):
+        do(q, lambda e: e.dma_start(out, in_), rd, wr, s, 16)
+
+    sent = [0]
+    nxt, prv = T.cores[(rank + 1) % N], T.cores[(rank - 1) % N]
+
+    def send(dst, s, outap, in_):
+        rid, pid = topo.addr(dst, core)
+        en = topo.engines(core, dst)[:8]
+        acc("gq", [in_[1]], [])
+        g.remote_dma(outap, in_[0], sem[s], sem.sent, pid, rid, sum(1 << e for e in en))
+        sent[0] += len(en)
+
+    def arrive(s, src, region):
+        note("rem", [], [region], s, len(topo.engines(src, core)[:8]), {})
+
+    dma("sy", T.NM[:, :], T.nm[:, :], "dm0", [], [("NM", 0, 256)])
+    dma("sy", T.PR[:, :], T.pr[:, :], "dm1", [], [("PR", 0, 256)])
+    dma("sy", T.ZL[:, 0:256], T.z0[:, :], "dm2", [], [("ZL", 0, 256)])
+    dma("sy", T.TH[:, :], T.th[:, :], "dm3", [], [("TH", 0, 5)])
+    dma("s", T.X[:, 0:2048], T.xt[:, :], "dx0", [], [("X", 0, 2048)])
+    ms(c("ONE"), 1.0)
+
+    def gi(out, pat, base, cm, flag=False):
+        if flag:
+            op("gq", lambda e: e.iota(out[0], pat, base, cm, allow_small_or_imprecise_dtypes=True), out)
+        else:
+            op("gq", lambda e: e.iota(out[0], pat, base, cm), out)
+
+    def gs(out, a, pat, cmp_, base, cm):
+        op("gq", lambda e: e.affine_select(out[0], a[0], pat, cmp_, 0.0, base, cm), out, a)
+
+    gi(c("PI"), [[0, 32]], 0, 1)
+    gi(c("DJ"), [[-1, 128]], 128, 1)
+    gs(c("BOa"), c("ONE"), [[-16, 8], [0, 16]], A.is_ge, 0, 1)
+    gs(c("BO"), c("BOa"), [[16, 8], [0, 16]], A.is_ge, 15, -1)
+    gs(c("If"), c("ONE"), [[-1, 128]], A.is_equal, 0, 1)
+    L3 = lambda b, s: (T[b][:, s], (b, s * 256, s * 256 + 256))
+    Lh = lambda b, s, h: (T[b][:, s, h, :], (b, s * 256 + h * 128, s * 256 + h * 128 + 128))
+    for h in range(2):
+        cp(Lh("LL", 0, h), c("NM", h * 128, h * 128 + 128))
+    gi(c("KR"), [[0, 24], [-1, 16]], 15, 0, True)
+    gi(c("RLi"), [[1, 24]], 0, 0)
+    gi(c("JI"), [[16, 8]], 0, 0)
+    for x4 in range(2):
+        gs((T.PX[:, x4, :], ("PX", x4 * 64, x4 * 64 + 64)), c("ONE", 0, 64), [[-32, 4], [-1, 16]], A.is_equal, -16 * x4, 1)
+    for t in range(1, N):
+        send(T.cores[(rank + t) % N], "l%d" % t, T.LL[:, t, :, :], L3("LL", 0))
+        arrive("l%d" % t, T.cores[(rank - t) % N], ("LL", t * 256, t * 256 + 256))
+    col = lambda j: c("COL", j, j + 1)
+    ts(c("NQH"), c("NM"), -2048, None, A.add)
+    ts(c("PT"), c("PR"), -1, 15, A.mult, A.add)
+    ts(c("PI2"), c("PI", 0, 16), 15, None, A.bitwise_and)
+    u0 = c("PI2", 0, 1)
+    ts(col(0), u0, 1, 0, A.mult, A.add)
+    ts(col(1), u0, -1, 15, A.mult, A.add)
+    ts(col(5), u0, -1, 15 - 32768, A.mult, A.add)
+    ms(c("COL", 15, 16), 128.0)
+    ts(c("DJ"), c("DJ"), 15, None, A.bitwise_and)
+    ts(c("DD"), c("DJ"), 0, None, A.is_equal)
+    cp(c("BOh"), c("BO")); cp(c("Ih"), c("If"))
+    for k in range(16):
+        ts(c("SEL", k * 128, k * 128 + 128), c("BOh"), c("DD", k, k + 1), None, A.mult)
+    sset = lambda t: 0 if t % N == 0 else 1 + t % 2
+
+    def statics(t):
+        s, ll = sset(t), L3("LL", t % N)
+        act(L3("OO", s), ll, F.Identity, bias=col(5), scale=16.0)
+        act(L3("A1", s), ll, F.Copy, bias=352.0)
+        act(L3("B1", s), ll, F.Copy, bias=1184.0)
+        for j, (w, k) in enumerate(((3232, 352), (2400, 1184))):
+            act((T.SXY[:, s, :, j, :], ("SXY", s * 512, s * 512 + 512)), ll, F.Copy, bias=float(w * k - 2 ** 23 - 13024 * 32), scale=float(w))
+
+    statics(0)
+    for k in range(16):
+        b = 512 * (k % 4)
+        mm(c("SB", b, b + 256), c("SEL", k * 128, k * 128 + 128), c("NQH"), True, True)
+        m, r = c("MSK", 256 * (k % 2), 256 * (k % 2) + 256), c("PRD", 256 * (k % 2), 256 * (k % 2) + 256)
+        ts(m, c("PT"), 15 - k, None, A.is_equal)
+        tt(r, m, c("SB", b, b + 256), A.mult)
+        mm(c("ST", 0, 256), c("Ih"), r, k == 0, k == 15)
+    ts(c("FMG"), c("PT"), col(1), None, A.is_equal)
+    cp(c("II", 0, 128), c("If")); cp(c("II", 128, 256), c("If"))
+    Ib = c("II", 0, 128)
+    ts(col(2), u0, -16, 240, A.mult, A.add)
+    ts(col(3), u0, -1, 16, A.mult, A.add)
+    ts(col(4), u0, 1, 1, A.mult, A.add)
+    ts(c("KDF", 0, 128), Ib, col(3), None, A.mult)
+    ts(c("KDF", 128, 256), Ib, col(4), None, A.mult)
+    ms(c("D0"), 0.0); ms(c("D0", 0, 256, 16), -1e9)
+    cp(c("RL"), c("RLi")); cp(c("BOb"), c("BO"))
+    ms(c("CM"), -128.0); ms(c("M3"), 0)
+    ms((T.PM[:, :, :, :, :], ("PM", 0, 512)), 0.0)
+    for i in range(4):
+        cp((T.PM[:, i, :, i % 2, :], ("PM", i * 128, i * 128 + 128)), (T.PX[:, i // 2, :], ("PX", 64 * (i // 2), 64 * (i // 2) + 64)))
+    ms(c("NC"), 0.0); ms(c("AT"), 0.0)
+    cp(c("LPi"), c("ST", 0, 256))
+    for h in range(2):
+        cp(c("PK", h * 512 + 384, h * 512 + 512), c("PT", h * 128, h * 128 + 128))
+    IND = c("BOb", 0, 128, 16)
+    half = lambda b, h, n=128: c(b, h * n, h * n + n)
+
+    def masks(h, P, i):
+        tt(c(P, i * 512, i * 512 + 384), ind(c("M3", h * 24, h * 24 + 24), c("RL")), c("KR"), A.is_equal)
+
+    def new_f(h, s, P, i):
+        mm(c("ST", 128, 256), c(P, i * 512 + 128, i * 512 + 256), Ib, True, True)
+        tt(c("MaL"), c("ST", 128, 256), Lh("LL", s[0], h), A.mult)
+        mm(c("ST", 384, 512), c("BO"), c("MaL"), True, False)
+        mm(c("ST", 384, 512), c("BOb"), c("CM"), False, True)
+
+    def names_to_H(h, s, H, i):
+        tt(c("PP", 128, 256), c("ST", 384, 512), Lh("B1", s[1], h), A.mult); yield
+        tt(c("PP", 0, 128), Lh("A1", s[1], h), half("LPi", h), A.mult); yield
+        q = s[1] * 512 + h * 256
+        tt(c("QQ"), c("PP"), (T.SXY[:, s[1], h, :, :], ("SXY", s[1] * 512, s[1] * 512 + 512)), A.add); yield
+        ts(c("HB"), c("QQ"), 65535, 5, A.bitwise_and, A.logical_shift_right); yield
+        cp(c("HF"), c("HB")); yield
+        op("v", lambda e: e.transpose(T[H][:, i, :, :], T.HF[:, :]), (None, (H, i * 256, i * 256 + 256)), c("HF")); yield
+
+    def first_state(h):
+        ts(c("T1", 0, 128), half("LPi", h), 16, None, A.mult); yield
+        mm(c("ST", 0, 256), c("FMG", h * 128, h * 128 + 128), c("KDF"), True, True)
+        tt(c("T1", 128, 256), c("T1", 0, 128), c("PT", h * 128, h * 128 + 128), A.add); yield
+        sc, r = h * 256, h * 160
+        scan(c("SC", sc, sc + 256), c("ST", 0, 256)); yield
+        ts(c("M3", h * 24 + 8, h * 24 + 16), c("SC", sc + 15, sc + 128, 16), -1, None, A.add); yield
+        ts(c("M3", h * 24 + 16, h * 24 + 24), c("SC", sc + 143, sc + 256, 16), -1, 16, A.mult, A.add); yield
+        masks(h, "PK", h); yield
+        new_f(h, (0, 0), "PK", h)
+        tt(c("RI", r, r + 128), c("T1", 128, 256), Lh("OO", 0, h), A.add); yield
+        for e in (128, 152):
+            cp(c("RI", r + e, r + e + 8), c("M3", h * 24 + 16, h * 24 + 24)); yield
+        for x in names_to_H(h, (0, 0), "HL", h):
+            yield
+
+    def lists(t, h):
+        i = t * 2 + h
+        for ib in range(4):
+            for x4 in range(2):
+                for g2 in range(2):
+                    w = ib * 32 + g2 * 16
+                    mm((T.HR[:, :, 2 * ib + x4:128:8], ("HR", 0, 1)), (T.PM[:, 2 * x4 + g2], ("PM", 0, 512)),
+                       (T.HL[:, i, :, w:w + 16], ("HL", i * 256, i * 256 + 256)), g2 == 0, g2 == 1)
+        ts(c("OFF", h * 256, h * 256 + 256), (T.HR[:, :, :], ("HR", 0, 1)), c("NC", t, t + 1), None, A.add)
+
+    XW = c("X", 0, 2112)
+
+    def raw(h, j):
+        return c("WW", h * 4096 + 512 * j, h * 4096 + 512 * j + 512) if j < 4 else c("XR", h * 2048 + 512 * (j - 4), h * 2048 + 512 * (j - 4) + 512)
+
+    def offs(h, j):
+        o = h * 256 + (128 + 32 * j if j < 4 else 32 * (j - 4))
+        return c("OFF", o, o + 32)
+
+    def gather(t, h, j):
+        if j in VSET[h]:
+            cp(raw(h, j), ind(XW, offs(h, j)))
+        else:
+            act(raw(h, j), ind(XW, offs(h, j)), F.Copy, bias=-128.0 if j < 4 else 0.0)
+
+    def minus_z(t, h, j):
+        b, i = 512 * (j % 4), t * 2 + h
+        mm(c("SB", b, b + 512), Ib, raw(h, j), True, False)
+        for r in range(4):
+            mm(c("SB", b + 128 * r, b + 128 * r + 128), c("nI"), c("ZL", i * 128, i * 128 + 128), False, r == 3)
+
+    def absval(h, j):
+        b = 512 * (j % 4)
+        if j < 4:
+            act(c("AY", h * 2048 + 512 * j, h * 2048 + 512 * j + 512), c("SB", b, b + 512), F.Abs, bias=c("COL", 15, 16))
+        else:
+            w = h * 4096 + 2048 + 512 * (j - 4)
+            act(c("WW", w, w + 512), c("SB", b, b + 512), F.Abs)
+
+    def sums(h, j):
+        for k in range(4 * (j % 4), 4 * (j % 4) + 4):
+            if j < 4:
+                mm(c("KP", 128 + k, 256, 16), c("AY", h * 2048 + k * 128, h * 2048 + k * 128 + 128), c("RX", 0, 8), False, False)
+            else:
+                w = h * 4096 + 2048 + k * 128
+                mm(c("KP", k, 256, 16), c("WW", w, w + 128), c("RX"), False, k == 15)
+
+    def keys0(t, h):
+        i = (t * 2 + h) * 512
+        kp = c("KP", 0, 256)
+        mm(kp, Ib, c("C2"), True, False)
+        mm(kp, c("OB"), c("KD"), False, False)
+        mm(c("KP", 128, 256), c("O5"), c("THD", t * 128, t * 128 + 128), False, False)
+        mm(kp, c("PK", i + 384, i + 512), c("II"), False, False)
+        for q in range(2):
+            for j in (128, 256):
+                mm(c("KP", q * 128, q * 128 + 128), c("PN"), c("PK", i + j, i + j + 128), False, False)
+
+    def select(t, h):
+        sc, e = h * 256, (t * 2 + h) * 32
+        scan(c("SC", sc, sc + 256), c("KP", 0, 256)); yield
+        mS, mD = c("SC", sc + 143, sc + 256, 16), c("SC", sc + 15, sc + 128, 16)
+        m, a, sel = c("TM", h * 16, h * 16 + 8), c("TM", 32 + h * 16, 40 + h * 16), c("SE", h * 8, h * 8 + 8)
+        ts(m, mS, 0, 2 ** 21, A.is_ge, A.mult); yield
+        tt(a, m, mS, A.add); yield
+        tt(sel, a, mD, A.max); yield
+        ts(half("KQ", h, 8), sel, 0x1F0, None, A.bitwise_and); yield
+        tt(half("GMx", h), ind(half("KQ", h, 8), c("RL", 0, 8)), c("M8"), A.mult); yield
+        mm(c("TL", 0, 8), Ib, c("JC"), True, False)
+        mm(c("TL", 0, 8), half("GMx", h), IND, False, True)
+        ts(c("ES", e, e + 32), ind(sel, c("RM")), 2 ** 21, None, A.is_lt); yield
+        ts(half("LS", h, 8), c("TL", 0, 8), 3968, None, A.add); yield
+        act(half("AW", h), ind(half("WW", h, 4096), half("LS", h, 8)), F.Abs)
+
+    def count_pe(t):
+        for j in range(2 * t + 2):
+            mm(c("TL", 24, 32), c("OB"), c("ES", j * 32, j * 32 + 8), j == 0, j == 2 * t + 1)
+
+    def count(t):
+        tt(c("DF", 48, 56), c("TL", 24, 32), c("BO", 0, 128, 16), A.mult); yield
+        op("v", lambda e: e.tensor_reduce(T.AT[:, t + 1:t + 2], T.DF[:, 48:56], AxisListType.X, A.add), c("AT", t + 1, t + 2), c("DF", 48, 56)); yield
+        if t + 1 < TS:
+            ts(c("AI", t, t + 1), c("AT", t + 1, t + 2), 1 / 64, -63 / 128, A.mult, A.add); yield
+            ts(c("NC", t + 1, t + 2), c("AI", t, t + 1), -64, c("AT", t + 1, t + 2), A.mult, A.add); yield
+
+    def pick(t, h):
+        i = t * 2 + h
+        z, zn = c("ZL", i * 128, i * 128 + 128), c("ZN", i * 128, i * 128 + 128)
+        tt(half("SZ", h), ind(half("WW", h, 4096), half("LS", h, 8)), z, A.add); yield
+        ts(half("HZ", h), half("SZ", h), 0.5, 63.75, A.mult, A.add); yield
+        tt(zn, half("HZ", h), half("AW", h), A.min); yield
+        if t + 1 < TS:
+            send(nxt, "az%d%d" % (t + 1, h), T.ZL[:, (i + 2) * 128:(i + 3) * 128], zn)
+            arrive("az%d%d" % (t + 1, h), prv, ("ZL", (i + 2) * 128, (i + 3) * 128))
+        mm(c("TL", 8, 16), zn, IND, True, True)
+        cp(c("UI", h * 16, h * 16 + 8), c("TL", 8, 16)); yield
+        ts(c("UI", h * 16 + 8, h * 16 + 16), c("UI", h * 16, h * 16 + 8), 7, None, A.bitwise_and); yield
+        tt(half("GMx", h), ind(c("UI", h * 16 + 8, h * 16 + 16), c("RL", 0, 8)), c("M1"), A.mult); yield
+        mm(c("TL", 16, 24), Ib, c("J8"), True, False)
+        mm(c("TL", 16, 24), half("GMx", h), IND, False, True)
+        cp(half("LC", h, 8), c("TL", 16, 24)); yield
+
+    def table(t, h):
+        i = t * 2 + h
+        zn, xw = c("ZN", i * 128, i * 128 + 128), c("X", 1024 * h, 1024 * h + 1024)
+        tt(half("SX2", h), ind(xw, half("LC", h, 8)), zn, A.add)
+        ts(half("HX2", h), half("SX2", h), 0.5, -0.25, A.mult, A.add)
+        cp(ind(xw, half("LC", h, 8)), half("HX2", h))
+        if h == 0 and t + 1 < TS:
+            cp(c("X", 2048, 2112), c("X", 0, 64))
+
+    def state(t, h):
+        i, s = t * 2 + h, (t % N, sset(t))
+        m, sel, e, b, j = h * 24, c("SE", h * 8, h * 8 + 8), i * 32, i * 160 + 128, i * 512
+        ts(c("RI", b + 8, b + 16), sel, 4, 15, A.logical_shift_right, A.bitwise_and); yield
+        ts(c("RI", b + 16, b + 24), sel, 15, None, A.bitwise_and); yield
+        tt(c("DF", 0, 24), c("RI", b, b + 24), c("RI", b + 8, b + 32), A.subtract); yield
+        tt(c("DF", 24, 48), c("DF", 0, 24), c("ES", e, e + 24), A.mult); yield
+        tt(c("M3", m, m + 24), c("RI", b + 8, b + 32), c("DF", 24, 48), A.add); yield
+        masks(h, "PS", i); yield
+        mm(c("ST", 0, 128), c("PS", j, j + 128), Ib, True, False)
+        mm(c("ST", 0, 128), c("PK", j + 128, j + 256), Ib, False, True)
+        tt(c("UO"), c("ST", 0, 128), Lh("OO", s[1], h), A.mult); yield
+        if t + 1 < TS:
+            new_f(h, s, "PS", i); yield
+        mm(c("ST", 256, 384), c("BO"), c("UO"), True, True)
+        R, Rn = c("RI", i * 160, i * 160 + 128), c("RS", i * 160, i * 160 + 128)
+        tt(c("R1"), c("ST", 256, 384), R, A.subtract); yield
+        tt(c("UR"), c("ST", 0, 128), c("R1"), A.mult); yield
+        tt(Rn, R, c("UR"), A.add); yield
+        tt(c("QI"), Rn, Lh("OO", s[1], h), A.subtract); yield
+        if t + 1 == TS:
+            ts(half("Pi", h), c("QI"), 15, None, A.bitwise_and); yield
+            return
+        ts(half("LPi", h), c("QI"), 4, None, A.arith_shift_right); yield
+        for x in names_to_H(h, s, "HN", i):
+            yield
+        n = i + 2
+
+        def ship(k, outap, inap, reg, lreg):
+            send(nxt, "a%s%d%d" % (k, t + 1, h), outap, (inap, reg))
+            arrive("a%s%d%d" % (k, t + 1, h), prv, lreg)
+        ship("h", T.HL[:, n, :, :], T.HN[:, i, :, :], ("HN", i * 256, i * 256 + 256), ("HL", n * 256, n * 256 + 256))
+        ts(half("Pi", h), c("QI"), 15, None, A.bitwise_and); yield
+        cp(c("PS", j + 384, j + 512), half("Pi", h)); yield
+        ship("p", T.PK[:, n * 512 + 128:n * 512 + 512], T.PS[:, j + 128:j + 512], ("PS", j + 128, j + 512), ("PK", n * 512 + 128, n * 512 + 512))
+        for x in (128, 152):
+            cp(c("RS", i * 160 + x, i * 160 + x + 8), c("M3", m + 16, m + 24)); yield
+        cp(c("RS", i * 160 + 136, i * 160 + 152), c("M3", m + 8, m + 24)); yield
+        ship("r", T.RI[:, n * 160:n * 160 + 160], T.RS[:, i * 160:i * 160 + 160], ("RS", i * 160, i * 160 + 160), ("RI", n * 160, n * 160 + 160))
+
+    def out(dst, src, q="sy"):
+        do(q, lambda e: e.dma_start(dst, src[0]), [src[1]], [], "out", 16)
+
+    def finish(h):
+        i = 2 * (TS - 1) + h
+        j = i * 512
+        cp(half("FA", h, 8), c("M3", h * 24 + 8, h * 24 + 16)); yield
+        mm(c("ST", 128, 256), c("PS", j + 128, j + 256), Ib, True, False)
+        mm(c("ST", 128, 256), c("PS", j + 256, j + 384), Ib, False, True)
+        o = (T.TL[0:8, 128:256], ("TL", 0, 1))
+        mm(o, half("FA", h, 8), Ib, True, True)
+        ts(c("P2", 0, 128), half("Pi", h), -1, col(1), A.mult, A.add); yield
+        tt(c("P2", 128, 256), c("ST", 128, 256), c("P2", 0, 128), A.mult); yield
+        y = (T.YF[0:8, h * 128:h * 128 + 128], ("YF", h * 128, h * 128 + 128))
+        ts(y, o, -1, 15, A.mult, A.add); yield
+        out(T.yf[:, h * 128:h * 128 + 128], y)
+        tt(c("P2", 0, 128), c("P2", 128, 256), half("Pi", h), A.add); yield
+        ts(half("YP", h), c("P2", 0, 128), -1, 15, A.mult, A.add); yield
+        out(T.yp[:, h * 128:h * 128 + 128], half("YP", h))
+
+    def chain(*gens):
+        for x in gens:
+            for y in x:
+                yield
+
+    def run(gen, n=10 ** 6):
+        for x in range(n):
+            try:
+                next(gen)
+            except StopIteration:
+                return
+
+    def mix(a, b):
+        for x in a:
+            yield
+            run(b, 1)
+        for x in b:
+            yield
+
+    def chunks(t, h, gen):
+        for j in range(8 + LAG):
+            if j < 8:
+                gather(t, h, j)
+                minus_z(t, h, j)
+            if j >= LAG:
+                absval(h, j - LAG)
+                sums(h, j - LAG)
+            run(gen, ADV[h])
+        run(gen)
+
+    run(first_state(0))
+    cp(c("X", 2048, 2112), c("X", 0, 64))
+    ts(c("nI"), Ib, -1, None, A.mult)
+    lists(0, 0)
+
+    def rest():
+        ts(c("PN"), Ib, -2 ** 25, None, A.mult); yield
+        ts(c("RX", 0, 8), IND, -512, None, A.mult); yield
+        ts(c("RX", 8, 16), IND, 512, None, A.mult); yield
+        for q in range(2):
+            ts(c("KD", q * 128, q * 128 + 128), Ib, col(2), None, A.mult); yield
+        ms(c("C2", 0, 128), 2.0 ** 20); ms(c("C2", 128, 256), 256.0)
+        ms(c("OB"), 1.0); ms(c("O5"), 512.0); yield
+        ts(c("COL", 8, 13), c("TH"), -1, -1, A.mult, A.add); yield
+        for t in range(TS):
+            ts(c("THD", t * 128, t * 128 + 128), c("Ih"), col(8 + t), None, A.mult); yield
+        ts(c("PI2", 2, 4), c("PI", 0, 2), 7, None, A.bitwise_and); yield
+        cp(c("RM"), c("PI2", 2, 4)); yield
+        ts(c("M8"), c("DD"), -8, None, A.mult); yield
+        cp(c("M1"), c("DD")); yield
+        ts(c("JC"), c("JI"), col(0), None, A.add); yield
+        ts(c("J8"), c("JC"), 8, None, A.mult); yield
+    run(rest())
+    for t in range(TS):
+        if t:
+            lists(t, 0)
+        keys0(t, 0)
+        chunks(t, 0, state(t - 1, 1) if t else first_state(1))
+        lists(t, 1)
+        if t in (1, 2, 3):
+            statics(t)
+        sel = select(t, 0)
+        run(sel, 1)
+        keys0(t, 1)
+        chunks(t, 1, chain(sel, pick(t, 0), state(t, 0), finish(0) if t + 1 == TS else ()))
+        table(t, 0)
+        run(select(t, 1))
+        count_pe(t)
+        run(mix(pick(t, 1), count(t)))
+        table(t, 1)
+    out(T.yx[:, :], c("X", 0, 2048))
+    out(T.yz[:, :], c("ZN", 8 * 128, 10 * 128), "s")
+    run(state(TS - 1, 1))
+    run(finish(1))
+    tt(c("YE"), c("AT", 1, 6), c("AT", 0, 5), A.subtract)
+    out(T.ye[:, :], c("YE"))
+    for s in cnt:
+        g.wait_ge(sem[s], cnt[s])
+    for t in range(1, N):
+        g.wait_ge(sem["l%d" % t], len(topo.engines(T.cores[(rank - t) % N], core)[:8]))
+    for t in range(1, TS):
+        for h in range(2):
+            for k in KINDS:
+                g.wait_ge(sem["a%s%d%d" % (k, t, h)], len(topo.engines(prv, core)[:8]))
+    g.wait_ge(sem.sent, sent[0])

@@ -1,13 +1,13 @@
 from concourse.mybir import dt, AluOpType as A, AxisListType, ActivationFunctionType as F
 
 N, TS = 4, 5
-VSET = ((7,), ())
-LAG = 2
-ADV = (5, 6)
+VPEN = 0.0
+WAKE, SHIP = 70.0, 4200.0
 SCRATCH = {
     "X": ("sbuf", [128, 2112], "bfloat16"), "NM": ("sbuf", [128, 256], "int32"), "PR": ("sbuf", [128, 256], "int32"),
     "TH": ("sbuf", [128, 5], "int32"), "LL": ("sbuf", [128, 4, 2, 128], "float32"), "NQH": ("sbuf", [128, 256], "float16"),
-    "PT": ("sbuf", [128, 256], "float16"), "FMG": ("sbuf", [128, 256], "bfloat16"),
+    "PT": ("sbuf", [128, 256], "bfloat16"), "MA": ("sbuf", [128, 512], "float32"), "MB": ("sbuf", [128, 2048], "bfloat16"),
+    "FMG": ("sbuf", [128, 256], "bfloat16"), "KC": ("sbuf", [128, 16], "float32"),
     "OO": ("sbuf", [128, 3, 2, 128], "float32"), "A1": ("sbuf", [128, 3, 2, 128], "float32"),
     "B1": ("sbuf", [128, 3, 2, 128], "float32"), "SXY": ("sbuf", [128, 3, 2, 2, 128], "float32"),
     "ONE": ("sbuf", [128, 128], "float32"), "If": ("sbuf", [128, 128], "float32"), "BOa": ("sbuf", [128, 128], "float32"),
@@ -28,16 +28,15 @@ SCRATCH = {
     "RI": ("sbuf", [128, 1600], "int32"), "RS": ("sbuf", [128, 1600], "int32"),
     "OFF": ("sbuf", [128, 512], "uint16"), "WW": ("sbuf", [128, 8192], "bfloat16"), "AY": ("sbuf", [128, 4096], "bfloat16"),
     "XR": ("sbuf", [128, 4096], "bfloat16"), "SC": ("sbuf", [128, 512], "float32"), "SE": ("sbuf", [128, 16], "int32"),
-    "TM": ("sbuf", [128, 64], "float32"), "KQ": ("sbuf", [128, 16], "int32"), "GMx": ("sbuf", [128, 256], "bfloat16"),
+    "TM": ("sbuf", [128, 64], "float32"), "KQ": ("sbuf", [128, 16], "int32"), "GMx": ("sbuf", [128, 512], "bfloat16"),
     "LS": ("sbuf", [128, 16], "uint16"), "LC": ("sbuf", [128, 16], "uint16"), "AW": ("sbuf", [128, 256], "bfloat16"),
     "SZ": ("sbuf", [128, 256], "float32"), "HZ": ("sbuf", [128, 256], "int32"), "UI": ("sbuf", [128, 32], "int32"),
     "SX2": ("sbuf", [128, 256], "float32"), "HX2": ("sbuf", [128, 256], "int32"), "ES": ("sbuf", [128, 320], "bfloat16"),
-    "M3": ("sbuf", [128, 48], "int32"), "DF": ("sbuf", [128, 96], "float32"),
+    "M3": ("sbuf", [128, 48], "int32"), "DF": ("sbuf", [128, 128], "float32"),
     "UO": ("sbuf", [128, 128], "float32"), "MaL": ("sbuf", [128, 128], "float32"), "R1": ("sbuf", [128, 128], "float32"),
-    "UR": ("sbuf", [128, 128], "float32"), "QI": ("sbuf", [128, 128], "int32"), "LPi": ("sbuf", [128, 256], "int32"),
-    "Pi": ("sbuf", [128, 256], "int32"), "PP": ("sbuf", [128, 256], "float32"), "QQ": ("sbuf", [128, 256], "int32"),
-    "HB": ("sbuf", [128, 256], "int32"), "HF": ("sbuf", [128, 256], "float16"),
-    "MSK": ("sbuf", [128, 512], "float16"), "PRD": ("sbuf", [128, 512], "float16"), "T1": ("sbuf", [128, 256], "float32"),
+    "QI2": ("sbuf", [128, 256], "float32"), "LPi": ("sbuf", [128, 256], "int32"), "Pi": ("sbuf", [128, 256], "int32"),
+    "QQ": ("sbuf", [128, 256], "int32"), "HB": ("sbuf", [128, 256], "int32"), "HF": ("sbuf", [128, 256], "float16"),
+    "MSK": ("sbuf", [128, 512], "bfloat16"), "PRD": ("sbuf", [128, 512], "float16"), "T1": ("sbuf", [128, 256], "float32"),
     "AT": ("sbuf", [128, 8], "float32"), "NC": ("sbuf", [128, 8], "float32"), "AI": ("sbuf", [128, 8], "int32"),
     "YE": ("sbuf", [128, 5], "float32"), "YP": ("sbuf", [128, 256], "float32"), "YF": ("sbuf", [128, 256], "float32"),
     "FA": ("sbuf", [128, 32], "bfloat16"), "P2": ("sbuf", [128, 256], "float32"),
@@ -56,33 +55,51 @@ def rank_program(g, core, T, topo):
         return
     sem = T.sem
     Q = {"v": g.vector, "p": g.tensor, "s": g.scalar, "gq": g, "sy": g.sync}
-    cnt, know, hist = {}, {q: {} for q in Q}, {}
+    cnt, know, hist, free, late = {}, {q: {} for q in Q}, {}, {q: 0.0 for q in Q}, [False]
 
-    def acc(q, rd, wr):
-        need = []
+    def needs(q, rd, wr):
+        out = []
         for regs, w in ((rd, False), (wr, True)):
             for (b, lo, hi) in regs:
                 for e in hist.get(b, ()):
                     if e[1] < hi and lo < e[2] and (w or e[3]) and not (e[0] == q and (q == "p" or not e[3])):
-                        need.append(e)
-        for e in sorted(need, key=lambda e: -e[5]):
+                        out.append(e)
+        return out
+
+    def start(d):
+        return max([free[d[0]]] + [e[7] + WAKE for e in needs(d[0], d[2], d[3])])
+
+    def acc(q, rd, wr):
+        for e in sorted(needs(q, rd, wr), key=lambda e: -e[5]):
             if know[q].get(e[4], 0) < e[5]:
                 Q[q].wait_ge(sem[e[4]], e[5])
                 for s, n in list(e[6].items()) + [(e[4], e[5])]:
                     know[q][s] = max(know[q].get(s, 0), n)
 
-    def note(q, rd, wr, s, n, snap):
+    def note(q, rd, wr, s, n, snap, fin):
         for regs, w in ((rd, False), (wr, True)):
             for (b, lo, hi) in regs:
                 old = [e for e in hist.get(b, []) if not (lo <= e[1] and e[2] <= hi and (w or (e[0] == q and not e[3])))]
-                hist[b] = old + [(q, lo, hi, w, s, n, snap)]
+                hist[b] = old + [(q, lo, hi, w, s, n, snap, fin)]
 
-    def do(q, fn, rd, wr, s=None, inc=1):
+    def do(d):
+        q, fn, rd, wr, s, inc, dur, lat, post = d
+        t0 = start(d)
         acc(q, rd, wr)
-        s = s or q
-        cnt[s] = cnt.get(s, 0) + inc
-        fn(Q[q]).then_inc(sem[s], inc)
-        note(q, rd, wr, s, cnt[s], dict(know[q]))
+        free[q] = t0 + dur
+        if s is None:
+            fn(Q[q])
+        else:
+            cnt[s] = cnt.get(s, 0) + inc
+            fn(Q[q]).then_inc(sem[s], inc)
+            note(q, rd, wr, s, cnt[s], dict(know[q]), t0 + dur + lat)
+        if post:
+            post(t0 + dur)
+
+    def give(d):
+        if late[0]:
+            return d
+        do(d)
 
     def ps(b, lo, hi):
         return (b, lo // 512, (hi + 511) // 512) if b in PSUM else (b, lo, hi)
@@ -94,53 +111,63 @@ def rank_program(g, core, T, topo):
     def ind(w, o):
         return (w[0].indirect(o[0]), w[1], o[1])
 
-    def op(q, fn, out, *ins):
+    def size(x):
+        n = 1
+        for k in list(x[0].shape)[1:]:
+            n *= int(k)
+        return n
+
+    def op(q, fn, out, *ins, dur=300.0):
         rs = [r for x in ins for r in x[1:]]
-        do(q, fn, [r for r in rs if r[0] not in PSUM], [out[1]] + [r for r in rs if r[0] in PSUM] + list(out[2:]))
+        return give((q, fn, [r for r in rs if r[0] not in PSUM], [out[1]] + [r for r in rs if r[0] in PSUM] + list(out[2:]), q, 1, dur, 0.0, None))
+
+    def span(n, f):
+        return max(64, f * n) + 60.0
 
     def tt(out, a, b, o):
-        op("v", lambda e: e.tensor_tensor(out[0], a[0], b[0], o), out, a, b)
+        n = size(b)
+        d = 60 + 1.56 * n if len(a) > 2 else span(n, 1 if a[1][0] in PSUM or b[1][0] in PSUM else 2)
+        return op("v", lambda e: e.tensor_tensor(out[0], a[0], b[0], o), out, a, b, dur=d)
 
     def ts(out, a, s1, s2, o0, o1=None):
         x = [s for s in (s1, s2) if isinstance(s, tuple)]
         f1, f2 = [s[0] if isinstance(s, tuple) else s for s in (s1, s2)]
+        d = span(size(out), 1)
         if o1 is None:
-            op("v", lambda e: e.tensor_scalar(out[0], a[0], f1, None, o0), out, a, *x)
-        else:
-            op("v", lambda e: e.tensor_scalar(out[0], a[0], f1, f2, o0, o1), out, a, *x)
+            return op("v", lambda e: e.tensor_scalar(out[0], a[0], f1, None, o0), out, a, *x, dur=d)
+        return op("v", lambda e: e.tensor_scalar(out[0], a[0], f1, f2, o0, o1), out, a, *x, dur=d)
 
     def cp(out, a):
-        op("v", lambda e: e.tensor_copy(out[0], a[0]), out, a)
+        d = 60 + 3.8 * size(a) if len(out) > 2 else (60 + 1.56 * size(out) if len(a) > 2 else span(size(out), 1))
+        return op("v", lambda e: e.tensor_copy(out[0], a[0]), out, a, dur=d)
 
     def ms(out, k):
-        op("v", lambda e: e.memset(out[0], k), out)
+        return op("v", lambda e: e.memset(out[0], k), out)
 
     def scan(out, d):
-        op("v", lambda e: e.tensor_tensor_scan(out[0], T.D0[:, :], d[0], 0.0, A.add, A.max), out, c("D0"), d)
+        return op("v", lambda e: e.tensor_tensor_scan(out[0], T.D0[:, :], d[0], 0.0, A.add, A.max), out, c("D0"), d, dur=320.0)
 
     def act(out, a, f, bias=0.0, scale=1.0):
-        x = [s for s in (bias,) if isinstance(s, tuple)]
-        bb = bias[0] if isinstance(bias, tuple) else bias
-        op("s", lambda e: e.activation(out[0], a[0], f, bias=bb, scale=scale), out, a, *x)
+        x = [s for s in (bias, scale) if isinstance(s, tuple)]
+        bb, sc = [s[0] if isinstance(s, tuple) else s for s in (bias, scale)]
+        return op("s", lambda e: e.activation(out[0], a[0], f, bias=bb, scale=sc), out, a, *x, dur=60 + (1.56 if len(a) > 2 else 1) * size(out))
 
-    def mm(out, l, r, start, stop):
-        op("p", lambda e: e.matmul(out[0], l[0], r[0], start, stop), out, l, r)
+    def mm(out, l, r, first, last):
+        d = max(64, size(r)) * (2.4 if l[1][0] in ("BO", "If") else 0.6)
+        return op("p", lambda e: e.matmul(out[0], l[0], r[0], first, last), out, l, r, dur=d)
 
     def dma(q, out, in_, s, rd, wr):
-        do(q, lambda e: e.dma_start(out, in_), rd, wr, s, 16)
+        return give((q, lambda e: e.dma_start(out, in_), rd, wr, s, 16, 60.0, 2200.0, None))
 
     sent = [0]
     nxt, prv = T.cores[(rank + 1) % N], T.cores[(rank - 1) % N]
 
-    def send(dst, s, outap, in_):
+    def send(dst, src, s, outap, in_, lreg):
         rid, pid = topo.addr(dst, core)
         en = topo.engines(core, dst)[:8]
-        acc("gq", [in_[1]], [])
-        g.remote_dma(outap, in_[0], sem[s], sem.sent, pid, rid, sum(1 << e for e in en))
         sent[0] += len(en)
-
-    def arrive(s, src, region):
-        note("rem", [], [region], s, len(topo.engines(src, core)[:8]), {})
+        return give(("gq", lambda e: e.remote_dma(outap, in_[0], sem[s], sem.sent, pid, rid, sum(1 << x for x in en)), [in_[1]], [], None, 0, 1000.0, 0.0,
+                     lambda t: note("rem", [], [lreg], s, len(topo.engines(src, core)[:8]), {}, t + SHIP - 1000)))
 
     dma("sy", T.NM[:, :], T.nm[:, :], "dm0", [], [("NM", 0, 256)])
     dma("sy", T.PR[:, :], T.pr[:, :], "dm1", [], [("PR", 0, 256)])
@@ -165,350 +192,438 @@ def rank_program(g, core, T, topo):
     gs(c("If"), c("ONE"), [[-1, 128]], A.is_equal, 0, 1)
     L3 = lambda b, s: (T[b][:, s], (b, s * 256, s * 256 + 256))
     Lh = lambda b, s, h: (T[b][:, s, h, :], (b, s * 256 + h * 128, s * 256 + h * 128 + 128))
+    half = lambda b, h, n=128: c(b, h * n, h * n + n)
+    col = lambda j: c("COL", j, j + 1)
     for h in range(2):
-        cp(Lh("LL", 0, h), c("NM", h * 128, h * 128 + 128))
+        cp(Lh("LL", 0, h), half("NM", h))
+    ts(c("PI2"), c("PI", 0, 16), 15, None, A.bitwise_and)
+    u0 = c("PI2", 0, 1)
+    ts(c("DJ"), c("DJ"), 15, None, A.bitwise_and)
+    ts(c("DD"), c("DJ"), 0, None, A.is_equal)
+    cp(c("BOh"), c("BO"))
+    ts(c("NQH"), c("NM"), -2048, None, A.add)
+    ts(c("PT"), c("PR"), -1, 15, A.mult, A.add)
     gi(c("KR"), [[0, 24], [-1, 16]], 15, 0, True)
     gi(c("RLi"), [[1, 24]], 0, 0)
     gi(c("JI"), [[16, 8]], 0, 0)
     for x4 in range(2):
         gs((T.PX[:, x4, :], ("PX", x4 * 64, x4 * 64 + 64)), c("ONE", 0, 64), [[-32, 4], [-1, 16]], A.is_equal, -16 * x4, 1)
     for t in range(1, N):
-        send(T.cores[(rank + t) % N], "l%d" % t, T.LL[:, t, :, :], L3("LL", 0))
-        arrive("l%d" % t, T.cores[(rank - t) % N], ("LL", t * 256, t * 256 + 256))
-    col = lambda j: c("COL", j, j + 1)
-    ts(c("NQH"), c("NM"), -2048, None, A.add)
-    ts(c("PT"), c("PR"), -1, 15, A.mult, A.add)
-    ts(c("PI2"), c("PI", 0, 16), 15, None, A.bitwise_and)
-    u0 = c("PI2", 0, 1)
-    ts(col(0), u0, 1, 0, A.mult, A.add)
-    ts(col(1), u0, -1, 15, A.mult, A.add)
-    ts(col(5), u0, -1, 15 - 32768, A.mult, A.add)
-    ms(c("COL", 15, 16), 128.0)
-    ts(c("DJ"), c("DJ"), 15, None, A.bitwise_and)
-    ts(c("DD"), c("DJ"), 0, None, A.is_equal)
-    cp(c("BOh"), c("BO")); cp(c("Ih"), c("If"))
-    for k in range(16):
-        ts(c("SEL", k * 128, k * 128 + 128), c("BOh"), c("DD", k, k + 1), None, A.mult)
+        send(T.cores[(rank + t) % N], T.cores[(rank - t) % N], "l%d" % t, T.LL[:, t, :, :], L3("LL", 0), ("LL", t * 256, t * 256 + 256))
     sset = lambda t: 0 if t % N == 0 else 1 + t % 2
+    ms(c("KC", 0, 1), 1.0)
+    late[0] = True
+    Ib, IND = c("II", 0, 128), c("BOb", 0, 128, 16)
 
     def statics(t):
+        if t == 3:
+            yield ("need", ("state", 1, 1))
+        if t:
+            yield ("need", ("sel", t - 1, 0))
+        yield ("need", "col")
         s, ll = sset(t), L3("LL", t % N)
-        act(L3("OO", s), ll, F.Identity, bias=col(5), scale=16.0)
-        act(L3("A1", s), ll, F.Copy, bias=352.0)
-        act(L3("B1", s), ll, F.Copy, bias=1184.0)
+        yield act(L3("OO", s), ll, F.Identity, bias=col(5), scale=16.0)
+        yield act(L3("A1", s), ll, F.Copy, bias=352.0)
+        yield act(L3("B1", s), ll, F.Copy, bias=1184.0)
         for j, (w, k) in enumerate(((3232, 352), (2400, 1184))):
-            act((T.SXY[:, s, :, j, :], ("SXY", s * 512, s * 512 + 512)), ll, F.Copy, bias=float(w * k - 2 ** 23 - 13024 * 32), scale=float(w))
+            yield act((T.SXY[:, s, :, j, :], ("SXY", s * 512, s * 512 + 512)), ll, F.Copy, bias=float(w * k - 2 ** 23 - 13024 * 32), scale=float(w))
+        yield ("done", ("statics", t))
 
-    statics(0)
-    for k in range(16):
-        b = 512 * (k % 4)
-        mm(c("SB", b, b + 256), c("SEL", k * 128, k * 128 + 128), c("NQH"), True, True)
-        m, r = c("MSK", 256 * (k % 2), 256 * (k % 2) + 256), c("PRD", 256 * (k % 2), 256 * (k % 2) + 256)
-        ts(m, c("PT"), 15 - k, None, A.is_equal)
-        tt(r, m, c("SB", b, b + 256), A.mult)
-        mm(c("ST", 0, 256), c("Ih"), r, k == 0, k == 15)
-    ts(c("FMG"), c("PT"), col(1), None, A.is_equal)
-    cp(c("II", 0, 128), c("If")); cp(c("II", 128, 256), c("If"))
-    Ib = c("II", 0, 128)
-    ts(col(2), u0, -16, 240, A.mult, A.add)
-    ts(col(3), u0, -1, 16, A.mult, A.add)
-    ts(col(4), u0, 1, 1, A.mult, A.add)
-    ts(c("KDF", 0, 128), Ib, col(3), None, A.mult)
-    ts(c("KDF", 128, 256), Ib, col(4), None, A.mult)
-    ms(c("D0"), 0.0); ms(c("D0", 0, 256, 16), -1e9)
-    cp(c("RL"), c("RLi")); cp(c("BOb"), c("BO"))
-    ms(c("CM"), -128.0); ms(c("M3"), 0)
-    ms((T.PM[:, :, :, :, :], ("PM", 0, 512)), 0.0)
-    for i in range(4):
-        cp((T.PM[:, i, :, i % 2, :], ("PM", i * 128, i * 128 + 128)), (T.PX[:, i // 2, :], ("PX", 64 * (i // 2), 64 * (i // 2) + 64)))
-    ms(c("NC"), 0.0); ms(c("AT"), 0.0)
-    cp(c("LPi"), c("ST", 0, 256))
-    for h in range(2):
-        cp(c("PK", h * 512 + 384, h * 512 + 512), c("PT", h * 128, h * 128 + 128))
-    IND = c("BOb", 0, 128, 16)
-    half = lambda b, h, n=128: c(b, h * n, h * n + n)
+    def rows_out():
+        for k in range(16):
+            b = 512 * (k % 4)
+            yield ts(c("SEL", k * 128, k * 128 + 128), c("BOh"), c("DD", k, k + 1), None, A.mult)
+            if k > 3:
+                yield ("need", ("kept", k - 4))
+            yield mm(c("SB", b, b + 256), c("SEL", k * 128, k * 128 + 128), c("NQH"), True, True)
+            yield ("done", ("row", k))
 
-    def masks(h, P, i):
-        tt(c(P, i * 512, i * 512 + 384), ind(c("M3", h * 24, h * 24 + 24), c("RL")), c("KR"), A.is_equal)
+    def some_masks():
+        for k in range(1, 16, 2):
+            a = c("MA", 256 * (k // 2 % 2), 256 * (k // 2 % 2) + 256)
+            yield ts(c("KC", k, k + 1), u0, 0, k - 15, A.mult, A.add)
+            yield act(a, c("PT"), F.Abs, bias=c("KC", k, k + 1))
+            yield act(c("MB", 256 * (k // 2), 256 * (k // 2) + 256), a, F.Relu, bias=c("KC", 0, 1), scale=-1.0)
+            yield ("done", ("mask", k))
+
+    def names():
+        yield cp(c("Ih"), c("If"))
+        for k in range(16):
+            b = 512 * (k % 4)
+            r = c("PRD", 256 * (k % 2), 256 * (k % 2) + 256)
+            if k % 2:
+                m = c("MB", 256 * (k // 2), 256 * (k // 2) + 256)
+                yield ("need", ("mask", k))
+            else:
+                m = c("MSK", 256 * (k // 2 % 2), 256 * (k // 2 % 2) + 256)
+                yield ts(m, c("PT"), 15 - k, None, A.is_equal)
+            yield ("need", ("row", k))
+            if k:
+                yield last
+            yield tt(r, m, c("SB", b, b + 256), A.mult)
+            yield ("done", ("kept", k))
+            last = mm(c("ST", 0, 256), c("Ih"), r, k == 0, k == 15)
+        yield last
+        yield cp(c("LPi"), c("ST", 0, 256))
+        yield ("done", "names")
+
+    def consts():
+        yield ts(col(0), u0, 1, 0, A.mult, A.add)
+        yield ts(col(1), u0, -1, 15, A.mult, A.add)
+        yield ts(col(5), u0, -1, 15 - 32768, A.mult, A.add)
+        yield ("done", "col")
+        yield ts(c("FMG"), c("PT"), col(1), None, A.is_equal)
+        for q in range(2):
+            yield act(c("II", q * 128, q * 128 + 128), c("If"), F.Copy)
+        yield ts(col(3), u0, -1, 16, A.mult, A.add)
+        yield ts(col(4), u0, 1, 1, A.mult, A.add)
+        for q in range(2):
+            yield act(c("KDF", q * 128, q * 128 + 128), c("If"), F.Copy, scale=col(3 + q))
+        yield ms(c("D0"), 0.0)
+        yield ms(c("D0", 0, 256, 16), -1e9)
+        yield cp(c("RL"), c("RLi"))
+        yield act(c("BOb"), c("BO"), F.Copy)
+        yield ms(c("CM"), -128.0)
+        yield ms(c("M3"), 0)
+        yield ms(c("NC"), 0.0)
+        yield ms(c("AT"), 0.0)
+        yield ms((T.PM[:, :, :, :, :], ("PM", 0, 512)), 0.0)
+        for i in range(4):
+            yield cp((T.PM[:, i, :, i % 2, :], ("PM", i * 128, i * 128 + 128)), (T.PX[:, i // 2, :], ("PX", 64 * (i // 2), 64 * (i // 2) + 64)))
+        yield act(c("nI"), c("If"), F.Copy, scale=-1.0)
+        yield ms(c("COL", 15, 16), 128.0)
+        yield ("done", "consts")
+        yield cp(c("X", 2048, 2112), c("X", 0, 64))
+        yield ("done", ("table", -1, 0))
+        yield ("done", ("table", -1, 1))
+        yield ("need", ("H", 0, 0))
+        for h in range(2):
+            yield cp(c("PK", h * 512 + 384, h * 512 + 512), half("PT", h))
+        yield act(c("PN"), c("If"), F.Copy, scale=-2.0 ** 25)
+        yield ts(c("RX", 0, 8), IND, -512, None, A.mult)
+        yield ts(c("RX", 8, 16), IND, 512, None, A.mult)
+        yield ts(col(2), u0, -16, 240, A.mult, A.add)
+        for q in range(2):
+            yield act(c("KD", q * 128, q * 128 + 128), c("If"), F.Copy, scale=col(2))
+            yield ms(c("C2", q * 128, q * 128 + 128), (2.0 ** 20, 256.0)[q])
+        yield ms(c("OB"), 1.0)
+        yield ms(c("O5"), 512.0)
+        yield ts(c("COL", 8, 13), c("TH"), -1, -1, A.mult, A.add)
+        for t in range(TS):
+            yield ts(c("THD", t * 128, t * 128 + 128), c("Ih"), col(8 + t), None, A.mult)
+        yield ("done", ("scan", -1, 1))
+        yield ts(c("PI2", 2, 4), c("PI", 0, 2), 7, None, A.bitwise_and)
+        yield cp(c("RM"), c("PI2", 2, 4))
+        yield act(c("M8"), c("DD"), F.Copy, scale=-8.0)
+        yield act(c("M1"), c("DD"), F.Copy)
+        yield ts(c("JC"), c("JI"), col(0), None, A.add)
+        yield ts(c("J8"), c("JC"), 8, None, A.mult)
+        yield ("done", "rest")
+
+    def masks(rows, P, i):
+        return tt(c(P, i * 512, i * 512 + 384), ind(rows, c("RL")), c("KR"), A.is_equal)
 
     def new_f(h, s, P, i):
-        mm(c("ST", 128, 256), c(P, i * 512 + 128, i * 512 + 256), Ib, True, True)
-        tt(c("MaL"), c("ST", 128, 256), Lh("LL", s[0], h), A.mult)
-        mm(c("ST", 384, 512), c("BO"), c("MaL"), True, False)
-        mm(c("ST", 384, 512), c("BOb"), c("CM"), False, True)
+        yield mm(c("ST", 128, 256), c(P, i * 512 + 128, i * 512 + 256), Ib, True, True)
+        yield tt(c("MaL"), c("ST", 128, 256), Lh("LL", s[0], h), A.mult)
+        yield [mm(c("ST", 384, 512), c("BO"), c("MaL"), True, False), mm(c("ST", 384, 512), c("BOb"), c("CM"), False, True)]
+        yield tt(c("ST", 128, 256), c("ST", 384, 512), Lh("B1", s[1], h), A.mult)
 
     def names_to_H(h, s, H, i):
-        tt(c("PP", 128, 256), c("ST", 384, 512), Lh("B1", s[1], h), A.mult); yield
-        tt(c("PP", 0, 128), Lh("A1", s[1], h), half("LPi", h), A.mult); yield
+        yield tt(c("ST", 0, 128), Lh("A1", s[1], h), half("LPi", h), A.mult)
         q = s[1] * 512 + h * 256
-        tt(c("QQ"), c("PP"), (T.SXY[:, s[1], h, :, :], ("SXY", s[1] * 512, s[1] * 512 + 512)), A.add); yield
-        ts(c("HB"), c("QQ"), 65535, 5, A.bitwise_and, A.logical_shift_right); yield
-        cp(c("HF"), c("HB")); yield
-        op("v", lambda e: e.transpose(T[H][:, i, :, :], T.HF[:, :]), (None, (H, i * 256, i * 256 + 256)), c("HF")); yield
+        yield tt(c("QQ"), c("ST", 0, 256), (T.SXY[:, s[1], h, :, :], ("SXY", s[1] * 512, s[1] * 512 + 512)), A.add)
+        yield ts(c("HB"), c("QQ"), 65535, 5, A.bitwise_and, A.logical_shift_right)
+        yield cp(c("HF"), c("HB"))
+        yield op("v", lambda e: e.transpose(T[H][:, i, :, :], T.HF[:, :]), (None, (H, i * 256, i * 256 + 256)), c("HF"), dur=190.0)
 
     def first_state(h):
-        ts(c("T1", 0, 128), half("LPi", h), 16, None, A.mult); yield
-        mm(c("ST", 0, 256), c("FMG", h * 128, h * 128 + 128), c("KDF"), True, True)
-        tt(c("T1", 128, 256), c("T1", 0, 128), c("PT", h * 128, h * 128 + 128), A.add); yield
+        if h:
+            yield ("need", ("state", -1, 0))
+        else:
+            for k in ("consts", "names", ("statics", 0)):
+                yield ("need", k)
+        yield mm(c("ST", 0, 256), half("FMG", h), c("KDF"), True, True)
         sc, r = h * 256, h * 160
-        scan(c("SC", sc, sc + 256), c("ST", 0, 256)); yield
-        ts(c("M3", h * 24 + 8, h * 24 + 16), c("SC", sc + 15, sc + 128, 16), -1, None, A.add); yield
-        ts(c("M3", h * 24 + 16, h * 24 + 24), c("SC", sc + 143, sc + 256, 16), -1, 16, A.mult, A.add); yield
-        masks(h, "PK", h); yield
-        new_f(h, (0, 0), "PK", h)
-        tt(c("RI", r, r + 128), c("T1", 128, 256), Lh("OO", 0, h), A.add); yield
-        for e in (128, 152):
-            cp(c("RI", r + e, r + e + 8), c("M3", h * 24 + 16, h * 24 + 24)); yield
+        yield ts(c("T1", 0, 128), half("LPi", h), 16, None, A.mult)
+        yield tt(c("RI", r, r + 128), c("T1", 0, 128), half("PT", h), A.add)
+        yield scan(c("SC", sc, sc + 256), c("ST", 0, 256))
+        yield ts(c("M3", h * 24 + 8, h * 24 + 16), c("SC", sc + 15, sc + 128, 16), -1, None, A.add)
+        yield ts(c("M3", h * 24 + 16, h * 24 + 24), c("SC", sc + 143, sc + 256, 16), -1, 16, A.mult, A.add)
+        yield masks(c("M3", h * 24, h * 24 + 24), "PK", h)
+        for x in new_f(h, (0, 0), "PK", h):
+            yield x
         for x in names_to_H(h, (0, 0), "HL", h):
-            yield
+            yield x
+        yield ("done", ("H", 0, h))
+        for e in (128, 152):
+            yield cp(c("RI", r + e, r + e + 8), c("M3", h * 24 + 16, h * 24 + 24))
+        for k in ("p", "r", "z"):
+            yield ("done", (k, 0, h))
+        yield ("done", ("state", -1, h))
 
     def lists(t, h):
         i = t * 2 + h
+        yield ("need", ("H", t, h))
+        yield ("need", ("scan", t - 1, 1))
+        if h:
+            yield ("need", ("L", t, 0))
         for ib in range(4):
+            p = []
             for x4 in range(2):
                 for g2 in range(2):
                     w = ib * 32 + g2 * 16
-                    mm((T.HR[:, :, 2 * ib + x4:128:8], ("HR", 0, 1)), (T.PM[:, 2 * x4 + g2], ("PM", 0, 512)),
-                       (T.HL[:, i, :, w:w + 16], ("HL", i * 256, i * 256 + 256)), g2 == 0, g2 == 1)
-        ts(c("OFF", h * 256, h * 256 + 256), (T.HR[:, :, :], ("HR", 0, 1)), c("NC", t, t + 1), None, A.add)
+                    p.append(mm((T.HR[:, :, 2 * ib + x4:128:8], ("HR", 0, 1)), (T.PM[:, 2 * x4 + g2], ("PM", 0, 512)),
+                                (T.HL[:, i, :, w:w + 16], ("HL", i * 256, i * 256 + 256)), g2 == 0, g2 == 1))
+            yield p
+        yield ("need", ("nc", t))
+        if h == 0:
+            yield ("need", ("g", t - 1, 0))
+        yield ts(c("OFF", h * 256, h * 256 + 256), (T.HR[:, :, :], ("HR", 0, 1)), c("NC", t, t + 1), None, A.add)
+        yield ("done", ("L", t, h))
 
     XW = c("X", 0, 2112)
 
     def raw(h, j):
         return c("WW", h * 4096 + 512 * j, h * 4096 + 512 * j + 512) if j < 4 else c("XR", h * 2048 + 512 * (j - 4), h * 2048 + 512 * (j - 4) + 512)
 
-    def offs(h, j):
-        o = h * 256 + (128 + 32 * j if j < 4 else 32 * (j - 4))
-        return c("OFF", o, o + 32)
-
-    def gather(t, h, j):
-        if j in VSET[h]:
-            cp(raw(h, j), ind(XW, offs(h, j)))
-        else:
-            act(raw(h, j), ind(XW, offs(h, j)), F.Copy, bias=-128.0 if j < 4 else 0.0)
-
-    def minus_z(t, h, j):
-        b, i = 512 * (j % 4), t * 2 + h
-        mm(c("SB", b, b + 512), Ib, raw(h, j), True, False)
-        for r in range(4):
-            mm(c("SB", b + 128 * r, b + 128 * r + 128), c("nI"), c("ZL", i * 128, i * 128 + 128), False, r == 3)
-
-    def absval(h, j):
-        b = 512 * (j % 4)
-        if j < 4:
-            act(c("AY", h * 2048 + 512 * j, h * 2048 + 512 * j + 512), c("SB", b, b + 512), F.Abs, bias=c("COL", 15, 16))
-        else:
-            w = h * 4096 + 2048 + 512 * (j - 4)
-            act(c("WW", w, w + 512), c("SB", b, b + 512), F.Abs)
-
-    def sums(h, j):
-        for k in range(4 * (j % 4), 4 * (j % 4) + 4):
+    def gathers(t, h):
+        yield ("need", ("L", t, h))
+        yield ("need", ("table", t - 1, 0))
+        yield ("need", ("table", t - 1, 1))
+        if h:
+            yield ("need", ("g", t, 0))
+        for j in range(8):
+            o = h * 256 + (128 + 32 * j if j < 4 else 32 * (j - 4))
+            w = ind(XW, c("OFF", o, o + 32))
+            a = act(raw(h, j), w, F.Copy, bias=-128.0 if j < 4 else 0.0)
             if j < 4:
-                mm(c("KP", 128 + k, 256, 16), c("AY", h * 2048 + k * 128, h * 2048 + k * 128 + 128), c("RX", 0, 8), False, False)
+                yield a
             else:
-                w = h * 4096 + 2048 + k * 128
-                mm(c("KP", k, 256, 16), c("WW", w, w + 128), c("RX"), False, k == 15)
+                yield ("alt", a, cp(raw(h, j), w))
+            yield ("done", ("g", t, h, j))
+        yield ("done", ("g", t, h))
 
-    def keys0(t, h):
+    def minus_z(t, h):
+        i = t * 2 + h
+        yield ("need", ("z", t, h))
+        for j in range(8):
+            b, J = 512 * (j % 4), i * 8 + j - 4
+            yield ("need", ("g", t, h, j))
+            if J >= 0:
+                yield ("need", ("abs", J))
+            yield [mm(c("SB", b, b + 512), Ib, raw(h, j), True, False)] + \
+                [mm(c("SB", b + 128 * r, b + 128 * r + 128), c("nI"), c("ZL", i * 128, i * 128 + 128), False, r == 3) for r in range(4)]
+            yield ("done", ("d", t, h, j))
+
+    def absval(t, h):
+        for j in range(8):
+            yield ("need", ("d", t, h, j))
+            b, w = 512 * (j % 4), h * 4096 + 2048 + 512 * (j - 4)
+            if j < 4:
+                yield act(c("AY", h * 2048 + 512 * j, h * 2048 + 512 * j + 512), c("SB", b, b + 512), F.Abs, bias=c("COL", 15, 16))
+            else:
+                yield act(c("WW", w, w + 512), c("SB", b, b + 512), F.Abs)
+            yield ("done", ("abs", (t * 2 + h) * 8 + j))
+
+    def sums(t, h):
         i = (t * 2 + h) * 512
+        yield ("need", ("scan", t - 1 + h, 1 - h))
+        yield ("need", ("p", t, h))
         kp = c("KP", 0, 256)
-        mm(kp, Ib, c("C2"), True, False)
-        mm(kp, c("OB"), c("KD"), False, False)
-        mm(c("KP", 128, 256), c("O5"), c("THD", t * 128, t * 128 + 128), False, False)
-        mm(kp, c("PK", i + 384, i + 512), c("II"), False, False)
-        for q in range(2):
-            for j in (128, 256):
-                mm(c("KP", q * 128, q * 128 + 128), c("PN"), c("PK", i + j, i + j + 128), False, False)
+        yield [mm(kp, Ib, c("C2"), True, False), mm(kp, c("OB"), c("KD"), False, False),
+               mm(c("KP", 128, 256), c("O5"), c("THD", t * 128, t * 128 + 128), False, False)]
+        yield [mm(kp, c("PK", i + 384, i + 512), c("II"), False, False)] + \
+            [mm(c("KP", q * 128, q * 128 + 128), c("PN"), c("PK", i + j, i + j + 128), False, False) for q in range(2) for j in (128, 256)]
+        for j in range(8):
+            yield ("need", ("abs", (t * 2 + h) * 8 + j))
+            p = []
+            for k in range(4 * (j % 4), 4 * (j % 4) + 4):
+                if j < 4:
+                    p.append(mm(c("KP", 128 + k, 256, 16), c("AY", h * 2048 + k * 128, h * 2048 + k * 128 + 128), c("RX", 0, 8), False, False))
+                else:
+                    w = h * 4096 + 2048 + k * 128
+                    p.append(mm(c("KP", k, 256, 16), c("WW", w, w + 128), c("RX"), False, k == 15))
+            yield p
+        yield ("done", ("sums", t, h))
 
-    def select(t, h):
-        sc, e = h * 256, (t * 2 + h) * 32
-        scan(c("SC", sc, sc + 256), c("KP", 0, 256)); yield
+    def choose(t, h):
+        sc, e, i = h * 256, (t * 2 + h) * 32, t * 2 + h
+        yield ("need", ("sums", t, h))
+        yield scan(c("SC", sc, sc + 256), c("KP", 0, 256))
+        yield ("done", ("scan", t, h))
+        yield ("need", "rest")
         mS, mD = c("SC", sc + 143, sc + 256, 16), c("SC", sc + 15, sc + 128, 16)
         m, a, sel = c("TM", h * 16, h * 16 + 8), c("TM", 32 + h * 16, 40 + h * 16), c("SE", h * 8, h * 8 + 8)
-        ts(m, mS, 0, 2 ** 21, A.is_ge, A.mult); yield
-        tt(a, m, mS, A.add); yield
-        tt(sel, a, mD, A.max); yield
-        ts(half("KQ", h, 8), sel, 0x1F0, None, A.bitwise_and); yield
-        tt(half("GMx", h), ind(half("KQ", h, 8), c("RL", 0, 8)), c("M8"), A.mult); yield
-        mm(c("TL", 0, 8), Ib, c("JC"), True, False)
-        mm(c("TL", 0, 8), half("GMx", h), IND, False, True)
-        ts(c("ES", e, e + 32), ind(sel, c("RM")), 2 ** 21, None, A.is_lt); yield
-        ts(half("LS", h, 8), c("TL", 0, 8), 3968, None, A.add); yield
-        act(half("AW", h), ind(half("WW", h, 4096), half("LS", h, 8)), F.Abs)
-
-    def count_pe(t):
-        for j in range(2 * t + 2):
-            mm(c("TL", 24, 32), c("OB"), c("ES", j * 32, j * 32 + 8), j == 0, j == 2 * t + 1)
+        yield ts(m, mS, 0, 2 ** 21, A.is_ge, A.mult)
+        yield tt(a, m, mS, A.add)
+        yield tt(sel, a, mD, A.max)
+        yield ts(half("KQ", h, 8), sel, 0x1F0, None, A.bitwise_and)
+        yield tt(half("GMx", h), ind(half("KQ", h, 8), c("RL", 0, 8)), c("M8"), A.mult)
+        yield [mm(c("TL", 0, 8), Ib, c("JC"), True, False), mm(c("TL", 0, 8), half("GMx", h), IND, False, True)]
+        yield ts(c("ES", e, e + 32), ind(sel, c("RM")), 2 ** 21, None, A.is_lt)
+        yield ("done", ("sel", t, h))
+        yield ts(half("LS", h, 8), c("TL", 0, 8), 3968, None, A.add)
+        yield act(half("AW", h), ind(half("WW", h, 4096), half("LS", h, 8)), F.Abs)
+        z, zn = c("ZL", i * 128, i * 128 + 128), c("ZN", i * 128, i * 128 + 128)
+        yield tt(half("SZ", h), ind(half("WW", h, 4096), half("LS", h, 8)), z, A.add)
+        yield ts(half("HZ", h), half("SZ", h), 0.5, 63.75, A.mult, A.add)
+        yield tt(zn, half("HZ", h), half("AW", h), A.min)
+        if t + 1 < TS:
+            n = (i + 2) * 128
+            yield send(nxt, prv, "az%d%d" % (t + 1, h), T.ZL[:, n:n + 128], zn, ("ZL", n, n + 128))
+            yield ("done", ("z", t + 1, h))
+        yield mm(c("TL", 8, 16), zn, IND, True, True)
+        yield cp(c("UI", h * 16, h * 16 + 8), c("TL", 8, 16))
+        yield ts(c("UI", h * 16 + 8, h * 16 + 16), c("UI", h * 16, h * 16 + 8), 7, None, A.bitwise_and)
+        yield tt(half("GMx", 2 + h), ind(c("UI", h * 16 + 8, h * 16 + 16), c("RL", 0, 8)), c("M1"), A.mult)
+        yield [mm(c("TL", 16, 24), Ib, c("J8"), True, False), mm(c("TL", 16, 24), half("GMx", 2 + h), IND, False, True)]
+        yield cp(half("LC", h, 8), c("TL", 16, 24))
+        xw = c("X", 1024 * h, 1024 * h + 1024)
+        yield tt(half("SX2", h), ind(xw, half("LC", h, 8)), zn, A.add)
+        yield ts(half("HX2", h), half("SX2", h), 0.5, -0.25, A.mult, A.add)
+        yield ("need", ("g", t, 1))
+        yield cp(ind(xw, half("LC", h, 8)), half("HX2", h))
+        if h == 0 and t + 1 < TS:
+            yield cp(c("X", 2048, 2112), c("X", 0, 64))
+        yield ("done", ("table", t, h))
 
     def count(t):
-        tt(c("DF", 48, 56), c("TL", 24, 32), c("BO", 0, 128, 16), A.mult); yield
-        op("v", lambda e: e.tensor_reduce(T.AT[:, t + 1:t + 2], T.DF[:, 48:56], AxisListType.X, A.add), c("AT", t + 1, t + 2), c("DF", 48, 56)); yield
+        yield ("need", ("sel", t, 0))
+        yield ("need", ("sel", t, 1))
+        yield [mm(c("TL", 24, 32), c("OB"), c("ES", j * 32, j * 32 + 8), j == 0, j == 2 * t + 1) for j in range(2 * t + 2)]
+        yield tt(c("DF", 96, 104), c("TL", 24, 32), c("BO", 0, 128, 16), A.mult)
+        yield op("v", lambda e: e.tensor_reduce(T.AT[:, t + 1:t + 2], T.DF[:, 96:104], AxisListType.X, A.add), c("AT", t + 1, t + 2), c("DF", 96, 104), dur=130.0)
         if t + 1 < TS:
-            ts(c("AI", t, t + 1), c("AT", t + 1, t + 2), 1 / 64, -63 / 128, A.mult, A.add); yield
-            ts(c("NC", t + 1, t + 2), c("AI", t, t + 1), -64, c("AT", t + 1, t + 2), A.mult, A.add); yield
-
-    def pick(t, h):
-        i = t * 2 + h
-        z, zn = c("ZL", i * 128, i * 128 + 128), c("ZN", i * 128, i * 128 + 128)
-        tt(half("SZ", h), ind(half("WW", h, 4096), half("LS", h, 8)), z, A.add); yield
-        ts(half("HZ", h), half("SZ", h), 0.5, 63.75, A.mult, A.add); yield
-        tt(zn, half("HZ", h), half("AW", h), A.min); yield
-        if t + 1 < TS:
-            send(nxt, "az%d%d" % (t + 1, h), T.ZL[:, (i + 2) * 128:(i + 3) * 128], zn)
-            arrive("az%d%d" % (t + 1, h), prv, ("ZL", (i + 2) * 128, (i + 3) * 128))
-        mm(c("TL", 8, 16), zn, IND, True, True)
-        cp(c("UI", h * 16, h * 16 + 8), c("TL", 8, 16)); yield
-        ts(c("UI", h * 16 + 8, h * 16 + 16), c("UI", h * 16, h * 16 + 8), 7, None, A.bitwise_and); yield
-        tt(half("GMx", h), ind(c("UI", h * 16 + 8, h * 16 + 16), c("RL", 0, 8)), c("M1"), A.mult); yield
-        mm(c("TL", 16, 24), Ib, c("J8"), True, False)
-        mm(c("TL", 16, 24), half("GMx", h), IND, False, True)
-        cp(half("LC", h, 8), c("TL", 16, 24)); yield
-
-    def table(t, h):
-        i = t * 2 + h
-        zn, xw = c("ZN", i * 128, i * 128 + 128), c("X", 1024 * h, 1024 * h + 1024)
-        tt(half("SX2", h), ind(xw, half("LC", h, 8)), zn, A.add)
-        ts(half("HX2", h), half("SX2", h), 0.5, -0.25, A.mult, A.add)
-        cp(ind(xw, half("LC", h, 8)), half("HX2", h))
-        if h == 0 and t + 1 < TS:
-            cp(c("X", 2048, 2112), c("X", 0, 64))
+            yield ts(c("AI", t, t + 1), c("AT", t + 1, t + 2), 1 / 64, -63 / 128, A.mult, A.add)
+            yield ts(c("NC", t + 1, t + 2), c("AI", t, t + 1), -64, c("AT", t + 1, t + 2), A.mult, A.add)
+            yield ("done", ("nc", t + 1))
+        else:
+            yield tt(c("YE"), c("AT", 1, 6), c("AT", 0, 5), A.subtract)
+            yield out(T.ye[:, :], c("YE"))
 
     def state(t, h):
-        i, s = t * 2 + h, (t % N, sset(t))
-        m, sel, e, b, j = h * 24, c("SE", h * 8, h * 8 + 8), i * 32, i * 160 + 128, i * 512
-        ts(c("RI", b + 8, b + 16), sel, 4, 15, A.logical_shift_right, A.bitwise_and); yield
-        ts(c("RI", b + 16, b + 24), sel, 15, None, A.bitwise_and); yield
-        tt(c("DF", 0, 24), c("RI", b, b + 24), c("RI", b + 8, b + 32), A.subtract); yield
-        tt(c("DF", 24, 48), c("DF", 0, 24), c("ES", e, e + 24), A.mult); yield
-        tt(c("M3", m, m + 24), c("RI", b + 8, b + 32), c("DF", 24, 48), A.add); yield
-        masks(h, "PS", i); yield
-        mm(c("ST", 0, 128), c("PS", j, j + 128), Ib, True, False)
-        mm(c("ST", 0, 128), c("PK", j + 128, j + 256), Ib, False, True)
-        tt(c("UO"), c("ST", 0, 128), Lh("OO", s[1], h), A.mult); yield
+        i, s, d = t * 2 + h, (t % N, sset(t)), 48 * h
+        sel, e, b, j = c("SE", h * 8, h * 8 + 8), i * 32, i * 160 + 128, i * 512
+        yield ("need", ("sel", t, h))
+        yield ("need", ("r", t, h))
+        yield ts(c("RI", b + 8, b + 16), sel, 4, 15, A.logical_shift_right, A.bitwise_and)
+        yield ts(c("RI", b + 16, b + 24), sel, 15, None, A.bitwise_and)
+        yield tt(c("DF", d, d + 24), c("RI", b, b + 24), c("RI", b + 8, b + 32), A.subtract)
+        yield tt(c("DF", d + 24, d + 48), c("DF", d, d + 24), c("ES", e, e + 24), A.mult)
+        yield tt(c("RS", b + 8, b + 32), c("RI", b + 8, b + 32), c("DF", d + 24, d + 48), A.add)
+        yield masks(c("RS", b + 8, b + 32), "PS", i)
+        yield ("need", ("statics", t % N))
+        Qo, Qn, R = c("RI", i * 160, i * 160 + 128), c("RS", i * 160, i * 160 + 128), half("QI2", h)
+        yield tt(R, Qo, Lh("OO", s[1], h), A.add)
+        yield ("need", ("state", t - 1 + h, 1 - h))
+        yield [mm(c("ST", 0, 128), c("PS", j, j + 128), Ib, True, False), mm(c("ST", 0, 128), c("PK", j + 128, j + 256), Ib, False, True)]
+        yield tt(c("UO"), c("ST", 0, 128), Lh("OO", s[1], h), A.mult)
+        yield mm(c("ST", 256, 384), c("BO"), c("UO"), True, True)
         if t + 1 < TS:
-            new_f(h, s, "PS", i); yield
-        mm(c("ST", 256, 384), c("BO"), c("UO"), True, True)
-        R, Rn = c("RI", i * 160, i * 160 + 128), c("RS", i * 160, i * 160 + 128)
-        tt(c("R1"), c("ST", 256, 384), R, A.subtract); yield
-        tt(c("UR"), c("ST", 0, 128), c("R1"), A.mult); yield
-        tt(Rn, R, c("UR"), A.add); yield
-        tt(c("QI"), Rn, Lh("OO", s[1], h), A.subtract); yield
+            for x in new_f(h, s, "PS", i):
+                yield x
+        yield tt(c("R1"), c("ST", 256, 384), R, A.subtract)
+        yield tt(c("ST", 256, 384), c("ST", 0, 128), c("R1"), A.mult)
+        yield tt(Qn, c("ST", 256, 384), Qo, A.add)
         if t + 1 == TS:
-            ts(half("Pi", h), c("QI"), 15, None, A.bitwise_and); yield
+            yield ts(half("Pi", h), Qn, 15, None, A.bitwise_and)
+            yield ("done", ("state", t, h))
             return
-        ts(half("LPi", h), c("QI"), 4, None, A.arith_shift_right); yield
+        yield ts(half("LPi", h), Qn, 4, None, A.arith_shift_right)
         for x in names_to_H(h, s, "HN", i):
-            yield
+            yield x
         n = i + 2
 
         def ship(k, outap, inap, reg, lreg):
-            send(nxt, "a%s%d%d" % (k, t + 1, h), outap, (inap, reg))
-            arrive("a%s%d%d" % (k, t + 1, h), prv, lreg)
-        ship("h", T.HL[:, n, :, :], T.HN[:, i, :, :], ("HN", i * 256, i * 256 + 256), ("HL", n * 256, n * 256 + 256))
-        ts(half("Pi", h), c("QI"), 15, None, A.bitwise_and); yield
-        cp(c("PS", j + 384, j + 512), half("Pi", h)); yield
-        ship("p", T.PK[:, n * 512 + 128:n * 512 + 512], T.PS[:, j + 128:j + 512], ("PS", j + 128, j + 512), ("PK", n * 512 + 128, n * 512 + 512))
-        for x in (128, 152):
-            cp(c("RS", i * 160 + x, i * 160 + x + 8), c("M3", m + 16, m + 24)); yield
-        cp(c("RS", i * 160 + 136, i * 160 + 152), c("M3", m + 8, m + 24)); yield
-        ship("r", T.RI[:, n * 160:n * 160 + 160], T.RS[:, i * 160:i * 160 + 160], ("RS", i * 160, i * 160 + 160), ("RI", n * 160, n * 160 + 160))
+            return send(nxt, prv, "a%s%d%d" % (k, t + 1, h), outap, (inap, reg), lreg)
+        yield ship("h", T.HL[:, n, :, :], T.HN[:, i, :, :], ("HN", i * 256, i * 256 + 256), ("HL", n * 256, n * 256 + 256))
+        yield ("done", ("H", t + 1, h))
+        yield ts(half("Pi", h), Qn, 15, None, A.bitwise_and)
+        yield cp(c("PS", j + 384, j + 512), half("Pi", h))
+        yield ship("p", T.PK[:, n * 512 + 128:n * 512 + 512], T.PS[:, j + 128:j + 512], ("PS", j + 128, j + 512), ("PK", n * 512 + 128, n * 512 + 512))
+        yield ("done", ("p", t + 1, h))
+        yield cp(c("RS", b, b + 8), c("RS", b + 24, b + 32))
+        yield ship("r", T.RI[:, n * 160:n * 160 + 160], T.RS[:, i * 160:i * 160 + 160], ("RS", i * 160, i * 160 + 160), ("RI", n * 160, n * 160 + 160))
+        yield ("done", ("r", t + 1, h))
+        yield ("done", ("state", t, h))
 
     def out(dst, src, q="sy"):
-        do(q, lambda e: e.dma_start(dst, src[0]), [src[1]], [], "out", 16)
+        return give((q, lambda e: e.dma_start(dst, src[0]), [src[1]], [], "out", 16, 60.0, 2200.0, None))
 
     def finish(h):
         i = 2 * (TS - 1) + h
         j = i * 512
-        cp(half("FA", h, 8), c("M3", h * 24 + 8, h * 24 + 16)); yield
-        mm(c("ST", 128, 256), c("PS", j + 128, j + 256), Ib, True, False)
-        mm(c("ST", 128, 256), c("PS", j + 256, j + 384), Ib, False, True)
-        o = (T.TL[0:8, 128:256], ("TL", 0, 1))
-        mm(o, half("FA", h, 8), Ib, True, True)
-        ts(c("P2", 0, 128), half("Pi", h), -1, col(1), A.mult, A.add); yield
-        tt(c("P2", 128, 256), c("ST", 128, 256), c("P2", 0, 128), A.mult); yield
+        yield ("need", ("state", TS - 1, h))
+        if h:
+            yield ("need", ("finish", 0))
+        yield cp(half("FA", h, 8), c("RS", i * 160 + 144, i * 160 + 152))
+        o = (T.ST[0:8, 384:512], ("ST", 0, 1))
+        yield [mm(c("ST", 128, 256), c("PS", j + 128, j + 256), Ib, True, False), mm(c("ST", 128, 256), c("PS", j + 256, j + 384), Ib, False, True),
+               mm(o, half("FA", h, 8), Ib, True, True)]
+        p = c("P2", 128 * h, 128 * h + 128)
+        yield ts(p, half("Pi", h), -1, col(1), A.mult, A.add)
+        yield tt(c("T1", 128 * h, 128 * h + 128), c("ST", 128, 256), p, A.mult)
         y = (T.YF[0:8, h * 128:h * 128 + 128], ("YF", h * 128, h * 128 + 128))
-        ts(y, o, -1, 15, A.mult, A.add); yield
-        out(T.yf[:, h * 128:h * 128 + 128], y)
-        tt(c("P2", 0, 128), c("P2", 128, 256), half("Pi", h), A.add); yield
-        ts(half("YP", h), c("P2", 0, 128), -1, 15, A.mult, A.add); yield
-        out(T.yp[:, h * 128:h * 128 + 128], half("YP", h))
+        yield ts(y, o, -1, 15, A.mult, A.add)
+        yield ("done", ("finish", h))
+        yield out(T.yf[:, h * 128:h * 128 + 128], y)
+        yield tt(p, c("T1", 128 * h, 128 * h + 128), half("Pi", h), A.add)
+        yield ts(half("YP", h), p, -1, 15, A.mult, A.add)
+        yield out(T.yp[:, h * 128:h * 128 + 128], half("YP", h))
 
-    def chain(*gens):
-        for x in gens:
-            for y in x:
-                yield
+    def last():
+        yield ("need", ("table", TS - 1, 0))
+        yield ("need", ("table", TS - 1, 1))
+        yield out(T.yx[:, :], c("X", 0, 2048))
+        yield out(T.yz[:, :], c("ZN", 8 * 128, 10 * 128), "s")
 
-    def run(gen, n=10 ** 6):
-        for x in range(n):
-            try:
-                next(gen)
-            except StopIteration:
+    th = [(0, some_masks()), (0, rows_out()), (0, names()), (2, consts()), (3, first_state(0)), (4, first_state(1)), (0, last())]
+    for t in range(TS):
+        for h in range(2):
+            th += [(0, lists(t, h)), (0, choose(t, h)), (3 - h, state(t, h)), (5, gathers(t, h)), (4, minus_z(t, h)), (4, absval(t, h)), (4, sums(t, h))]
+        th.append((1, count(t)))
+        if t < N:
+            th.append((6, statics(t)))
+    for h in range(2):
+        th.append((3, finish(h)))
+    ev, live, blocked = {("nc", 0), ("g", -1, 0)}, [], {}
+
+    def pull(rec):
+        for x in rec[1]:
+            if isinstance(x, tuple) and x[0] == "done":
+                ev.add(x[1])
+                for r in blocked.pop(x[1], ()):
+                    pull(r)
+            elif isinstance(x, tuple) and x[0] == "need":
+                if x[1] not in ev:
+                    blocked.setdefault(x[1], []).append(rec)
+                    return
+            else:
+                rec[2] = x
+                live.append(rec)
                 return
 
-    def mix(a, b):
-        for x in a:
-            yield
-            run(b, 1)
-        for x in b:
-            yield
+    def when(x):
+        if isinstance(x, list):
+            return start(x[0]), x
+        if x[0] == "alt":
+            a, v = start(x[1]), start(x[2])
+            return (v, [x[2]]) if v + x[2][6] + VPEN < a + x[1][6] else (a, [x[1]])
+        return start(x), [x]
 
-    def chunks(t, h, gen):
-        for j in range(8 + LAG):
-            if j < 8:
-                gather(t, h, j)
-                minus_z(t, h, j)
-            if j >= LAG:
-                absval(h, j - LAG)
-                sums(h, j - LAG)
-            run(gen, ADV[h])
-        run(gen)
-
-    run(first_state(0))
-    cp(c("X", 2048, 2112), c("X", 0, 64))
-    ts(c("nI"), Ib, -1, None, A.mult)
-    lists(0, 0)
-
-    def rest():
-        ts(c("PN"), Ib, -2 ** 25, None, A.mult); yield
-        ts(c("RX", 0, 8), IND, -512, None, A.mult); yield
-        ts(c("RX", 8, 16), IND, 512, None, A.mult); yield
-        for q in range(2):
-            ts(c("KD", q * 128, q * 128 + 128), Ib, col(2), None, A.mult); yield
-        ms(c("C2", 0, 128), 2.0 ** 20); ms(c("C2", 128, 256), 256.0)
-        ms(c("OB"), 1.0); ms(c("O5"), 512.0); yield
-        ts(c("COL", 8, 13), c("TH"), -1, -1, A.mult, A.add); yield
-        for t in range(TS):
-            ts(c("THD", t * 128, t * 128 + 128), c("Ih"), col(8 + t), None, A.mult); yield
-        ts(c("PI2", 2, 4), c("PI", 0, 2), 7, None, A.bitwise_and); yield
-        cp(c("RM"), c("PI2", 2, 4)); yield
-        ts(c("M8"), c("DD"), -8, None, A.mult); yield
-        cp(c("M1"), c("DD")); yield
-        ts(c("JC"), c("JI"), col(0), None, A.add); yield
-        ts(c("J8"), c("JC"), 8, None, A.mult); yield
-    run(rest())
-    for t in range(TS):
-        if t:
-            lists(t, 0)
-        keys0(t, 0)
-        chunks(t, 0, state(t - 1, 1) if t else first_state(1))
-        lists(t, 1)
-        if t in (1, 2, 3):
-            statics(t)
-        sel = select(t, 0)
-        run(sel, 1)
-        keys0(t, 1)
-        chunks(t, 1, chain(sel, pick(t, 0), state(t, 0), finish(0) if t + 1 == TS else ()))
-        table(t, 0)
-        run(select(t, 1))
-        count_pe(t)
-        run(mix(pick(t, 1), count(t)))
-        table(t, 1)
-    out(T.yx[:, :], c("X", 0, 2048))
-    out(T.yz[:, :], c("ZN", 8 * 128, 10 * 128), "s")
-    run(state(TS - 1, 1))
-    run(finish(1))
-    tt(c("YE"), c("AT", 1, 6), c("AT", 0, 5), A.subtract)
-    out(T.ye[:, :], c("YE"))
+    for n, (p, gen) in enumerate(th):
+        pull([p * 1000 + n, gen, None])
+    while live:
+        best = None
+        for rec in live:
+            s, calls = when(rec[2])
+            if best is None or (s, rec[0]) < (best[0], best[1][0]):
+                best = (s, rec, calls)
+        live.remove(best[1])
+        for d in best[2]:
+            do(d)
+        pull(best[1])
     for s in cnt:
         g.wait_ge(sem[s], cnt[s])
     for t in range(1, N):

from concourse.mybir import dt, AluOpType as A, AxisListType, ActivationFunctionType as F

N, TS = 4, 5
VPEN = 0.0
WAKE, SHIP = 70.0, 4200.0
SCRATCH = {
    "X": ("sbuf", [128, 2112], "bfloat16"), "NM": ("sbuf", [128, 256], "int32"), "PR": ("sbuf", [128, 256], "int32"),
    "TH": ("sbuf", [128, 5], "int32"), "LL": ("sbuf", [128, 4, 2, 128], "float32"), "NQH": ("sbuf", [128, 256], "float16"),
    "PT": ("sbuf", [128, 256], "bfloat16"), "MA": ("sbuf", [128, 512], "float32"), "MB": ("sbuf", [128, 2048], "bfloat16"),
    "FMG": ("sbuf", [128, 256], "bfloat16"), "KC": ("sbuf", [128, 16], "float32"),
    "OO": ("sbuf", [128, 3, 2, 128], "float32"), "A1": ("sbuf", [128, 3, 2, 128], "float32"),
    "B1": ("sbuf", [128, 3, 2, 128], "float32"), "SXY": ("sbuf", [128, 3, 2, 2, 128], "float32"),
    "ONE": ("sbuf", [128, 128], "float32"), "If": ("sbuf", [128, 128], "float32"), "BOa": ("sbuf", [128, 128], "float32"),
    "BO": ("sbuf", [128, 128], "float32"), "PX": ("sbuf", [128, 2, 64], "float32"), "PM": ("sbuf", [128, 4, 4, 2, 16], "float16"),
    "II": ("sbuf", [128, 256], "bfloat16"), "nI": ("sbuf", [128, 128], "bfloat16"), "PN": ("sbuf", [128, 128], "bfloat16"),
    "Ih": ("sbuf", [128, 128], "float16"), "BOb": ("sbuf", [128, 128], "bfloat16"), "BOh": ("sbuf", [128, 128], "float16"),
    "SEL": ("sbuf", [128, 2048], "float16"), "RX": ("sbuf", [128, 16], "bfloat16"), "KD": ("sbuf", [128, 256], "bfloat16"),
    "KDF": ("sbuf", [128, 256], "bfloat16"), "C2": ("sbuf", [128, 256], "bfloat16"), "OB": ("sbuf", [128, 128], "bfloat16"),
    "O5": ("sbuf", [128, 128], "float16"), "THD": ("sbuf", [128, 640], "float16"), "D0": ("sbuf", [128, 256], "float32"),
    "RLi": ("sbuf", [128, 24], "int32"), "RL": ("sbuf", [128, 24], "uint16"), "PI": ("sbuf", [128, 32], "int32"),
    "RM": ("sbuf", [128, 2], "uint16"), "DJ": ("sbuf", [128, 128], "int32"), "DD": ("sbuf", [128, 128], "float32"),
    "M8": ("sbuf", [128, 128], "bfloat16"), "M1": ("sbuf", [128, 128], "bfloat16"), "JI": ("sbuf", [128, 8], "int32"),
    "JC": ("sbuf", [128, 8], "bfloat16"), "J8": ("sbuf", [128, 8], "bfloat16"), "KR": ("sbuf", [128, 384], "bfloat16"),
    "CM": ("sbuf", [128, 128], "bfloat16"), "COL": ("sbuf", [128, 16], "float32"), "PI2": ("sbuf", [128, 16], "int32"),
    "ZL": ("sbuf", [128, 1280], "bfloat16"), "ZN": ("sbuf", [128, 1280], "bfloat16"),
    "HL": ("sbuf", [128, 10, 2, 128], "float16"), "HN": ("sbuf", [128, 10, 2, 128], "float16"),
    "PK": ("sbuf", [128, 5120], "bfloat16"), "PS": ("sbuf", [128, 5120], "bfloat16"),
    "RI": ("sbuf", [128, 1600], "int32"), "RS": ("sbuf", [128, 1600], "int32"),
    "OFF": ("sbuf", [128, 512], "uint16"), "WW": ("sbuf", [128, 8192], "bfloat16"), "AY": ("sbuf", [128, 4096], "bfloat16"),
    "XR": ("sbuf", [128, 4096], "bfloat16"), "SC": ("sbuf", [128, 512], "float32"), "SE": ("sbuf", [128, 16], "int32"),
    "TM": ("sbuf", [128, 64], "float32"), "KQ": ("sbuf", [128, 16], "int32"), "GMx": ("sbuf", [128, 512], "bfloat16"),
    "LS": ("sbuf", [128, 16], "uint16"), "LC": ("sbuf", [128, 16], "uint16"), "AW": ("sbuf", [128, 256], "bfloat16"),
    "SZ": ("sbuf", [128, 256], "float32"), "HZ": ("sbuf", [128, 256], "int32"), "UI": ("sbuf", [128, 32], "int32"),
    "SX2": ("sbuf", [128, 256], "float32"), "HX2": ("sbuf", [128, 256], "int32"), "ES": ("sbuf", [128, 320], "bfloat16"),
    "M3": ("sbuf", [128, 48], "int32"), "DF": ("sbuf", [128, 128], "float32"),
    "UO": ("sbuf", [128, 128], "float32"), "MaL": ("sbuf", [128, 128], "float32"), "R1": ("sbuf", [128, 128], "float32"),
    "QI2": ("sbuf", [128, 256], "float32"), "LPi": ("sbuf", [128, 256], "int32"), "Pi": ("sbuf", [128, 256], "int32"),
    "QQ": ("sbuf", [128, 256], "int32"), "HB": ("sbuf", [128, 256], "int32"), "HF": ("sbuf", [128, 256], "float16"),
    "MSK": ("sbuf", [128, 512], "bfloat16"), "PRD": ("sbuf", [128, 512], "float16"), "T1": ("sbuf", [128, 256], "float32"),
    "AT": ("sbuf", [128, 8], "float32"), "NC": ("sbuf", [128, 8], "float32"), "AI": ("sbuf", [128, 8], "int32"),
    "YE": ("sbuf", [128, 5], "float32"), "YP": ("sbuf", [128, 256], "float32"), "YF": ("sbuf", [128, 256], "float32"),
    "FA": ("sbuf", [128, 32], "bfloat16"), "P2": ("sbuf", [128, 256], "float32"),
    "SB": ("psum", [128, 2048], "float32"), "KP": ("psum", [128, 512], "float32"), "HR": ("psum", [128, 2, 128], "float32"),
    "ST": ("psum", [128, 512], "float32"), "TL": ("psum", [128, 512], "float32"),
}
PSUM = ("SB", "KP", "ST", "TL", "HR")
KINDS = ("z", "h", "p", "r")
SEMAPHORES = ["v", "p", "s", "gq", "sent", "dm0", "dm1", "dm2", "dm3", "dx0", "out"] + \
    ["a%s%d%d" % (k, t, h) for t in range(1, TS) for h in range(2) for k in KINDS] + ["l%d" % t for t in range(1, N)]


def rank_program(g, core, T, topo):
    rank = T.rank_of(core)
    if rank is None:
        return
    sem = T.sem
    Q = {"v": g.vector, "p": g.tensor, "s": g.scalar, "gq": g, "sy": g.sync}
    cnt, know, hist, free, late = {}, {q: {} for q in Q}, {}, {q: 0.0 for q in Q}, [False]

    def needs(q, rd, wr):
        out = []
        for regs, w in ((rd, False), (wr, True)):
            for (b, lo, hi) in regs:
                for e in hist.get(b, ()):
                    if e[1] < hi and lo < e[2] and (w or e[3]) and not (e[0] == q and (q == "p" or not e[3])):
                        out.append(e)
        return out

    def start(d):
        return max([free[d[0]]] + [e[7] + WAKE for e in needs(d[0], d[2], d[3])])

    def acc(q, rd, wr):
        for e in sorted(needs(q, rd, wr), key=lambda e: -e[5]):
            if know[q].get(e[4], 0) < e[5]:
                Q[q].wait_ge(sem[e[4]], e[5])
                for s, n in list(e[6].items()) + [(e[4], e[5])]:
                    know[q][s] = max(know[q].get(s, 0), n)

    def note(q, rd, wr, s, n, snap, fin):
        for regs, w in ((rd, False), (wr, True)):
            for (b, lo, hi) in regs:
                old = [e for e in hist.get(b, []) if not (lo <= e[1] and e[2] <= hi and (w or (e[0] == q and not e[3])))]
                hist[b] = old + [(q, lo, hi, w, s, n, snap, fin)]

    def do(d):
        q, fn, rd, wr, s, inc, dur, lat, post = d
        t0 = start(d)
        acc(q, rd, wr)
        free[q] = t0 + dur
        if s is None:
            fn(Q[q])
        else:
            cnt[s] = cnt.get(s, 0) + inc
            fn(Q[q]).then_inc(sem[s], inc)
            note(q, rd, wr, s, cnt[s], dict(know[q]), t0 + dur + lat)
        if post:
            post(t0 + dur)

    def give(d):
        if late[0]:
            return d
        do(d)

    def ps(b, lo, hi):
        return (b, lo // 512, (hi + 511) // 512) if b in PSUM else (b, lo, hi)

    def c(b, lo=0, hi=None, st=1):
        hi = T[b].shape[1] if hi is None else hi
        return (T[b][:, lo:hi:st], ps(b, lo, hi))

    def ind(w, o):
        return (w[0].indirect(o[0]), w[1], o[1])

    def size(x):
        n = 1
        for k in list(x[0].shape)[1:]:
            n *= int(k)
        return n

    def op(q, fn, out, *ins, dur=300.0):
        rs = [r for x in ins for r in x[1:]]
        return give((q, fn, [r for r in rs if r[0] not in PSUM], [out[1]] + [r for r in rs if r[0] in PSUM] + list(out[2:]), q, 1, dur, 0.0, None))

    def span(n, f):
        return max(64, f * n) + 60.0

    def tt(out, a, b, o):
        n = size(b)
        d = 60 + 1.56 * n if len(a) > 2 else span(n, 1 if a[1][0] in PSUM or b[1][0] in PSUM else 2)
        return op("v", lambda e: e.tensor_tensor(out[0], a[0], b[0], o), out, a, b, dur=d)

    def ts(out, a, s1, s2, o0, o1=None):
        x = [s for s in (s1, s2) if isinstance(s, tuple)]
        f1, f2 = [s[0] if isinstance(s, tuple) else s for s in (s1, s2)]
        d = span(size(out), 1)
        if o1 is None:
            return op("v", lambda e: e.tensor_scalar(out[0], a[0], f1, None, o0), out, a, *x, dur=d)
        return op("v", lambda e: e.tensor_scalar(out[0], a[0], f1, f2, o0, o1), out, a, *x, dur=d)

    def cp(out, a):
        d = 60 + 3.8 * size(a) if len(out) > 2 else (60 + 1.56 * size(out) if len(a) > 2 else span(size(out), 1))
        return op("v", lambda e: e.tensor_copy(out[0], a[0]), out, a, dur=d)

    def ms(out, k):
        return op("v", lambda e: e.memset(out[0], k), out)

    def scan(out, d):
        return op("v", lambda e: e.tensor_tensor_scan(out[0], T.D0[:, :], d[0], 0.0, A.add, A.max), out, c("D0"), d, dur=320.0)

    def act(out, a, f, bias=0.0, scale=1.0):
        x = [s for s in (bias, scale) if isinstance(s, tuple)]
        bb, sc = [s[0] if isinstance(s, tuple) else s for s in (bias, scale)]
        return op("s", lambda e: e.activation(out[0], a[0], f, bias=bb, scale=sc), out, a, *x, dur=60 + (1.56 if len(a) > 2 else 1) * size(out))

    def mm(out, l, r, first, last):
        d = max(64, size(r)) * (2.4 if l[1][0] in ("BO", "If") else 0.6)
        return op("p", lambda e: e.matmul(out[0], l[0], r[0], first, last), out, l, r, dur=d)

    def dma(q, out, in_, s, rd, wr):
        return give((q, lambda e: e.dma_start(out, in_), rd, wr, s, 16, 60.0, 2200.0, None))

    sent = [0]
    nxt, prv = T.cores[(rank + 1) % N], T.cores[(rank - 1) % N]

    def send(dst, src, s, outap, in_, lreg):
        rid, pid = topo.addr(dst, core)
        en = topo.engines(core, dst)[:8]
        sent[0] += len(en)
        return give(("gq", lambda e: e.remote_dma(outap, in_[0], sem[s], sem.sent, pid, rid, sum(1 << x for x in en)), [in_[1]], [], None, 0, 1000.0, 0.0,
                     lambda t: note("rem", [], [lreg], s, len(topo.engines(src, core)[:8]), {}, t + SHIP - 1000)))

    dma("sy", T.NM[:, :], T.nm[:, :], "dm0", [], [("NM", 0, 256)])
    dma("sy", T.PR[:, :], T.pr[:, :], "dm1", [], [("PR", 0, 256)])
    dma("sy", T.ZL[:, 0:256], T.z0[:, :], "dm2", [], [("ZL", 0, 256)])
    dma("sy", T.TH[:, :], T.th[:, :], "dm3", [], [("TH", 0, 5)])
    dma("s", T.X[:, 0:2048], T.xt[:, :], "dx0", [], [("X", 0, 2048)])
    ms(c("ONE"), 1.0)

    def gi(out, pat, base, cm, flag=False):
        if flag:
            op("gq", lambda e: e.iota(out[0], pat, base, cm, allow_small_or_imprecise_dtypes=True), out)
        else:
            op("gq", lambda e: e.iota(out[0], pat, base, cm), out)

    def gs(out, a, pat, cmp_, base, cm):
        op("gq", lambda e: e.affine_select(out[0], a[0], pat, cmp_, 0.0, base, cm), out, a)

    gi(c("PI"), [[0, 32]], 0, 1)
    gi(c("DJ"), [[-1, 128]], 128, 1)
    gs(c("BOa"), c("ONE"), [[-16, 8], [0, 16]], A.is_ge, 0, 1)
    gs(c("BO"), c("BOa"), [[16, 8], [0, 16]], A.is_ge, 15, -1)
    gs(c("If"), c("ONE"), [[-1, 128]], A.is_equal, 0, 1)
    L3 = lambda b, s: (T[b][:, s], (b, s * 256, s * 256 + 256))
    Lh = lambda b, s, h: (T[b][:, s, h, :], (b, s * 256 + h * 128, s * 256 + h * 128 + 128))
    half = lambda b, h, n=128: c(b, h * n, h * n + n)
    col = lambda j: c("COL", j, j + 1)
    for h in range(2):
        cp(Lh("LL", 0, h), half("NM", h))
    ts(c("PI2"), c("PI", 0, 16), 15, None, A.bitwise_and)
    u0 = c("PI2", 0, 1)
    ts(c("DJ"), c("DJ"), 15, None, A.bitwise_and)
    ts(c("DD"), c("DJ"), 0, None, A.is_equal)
    cp(c("BOh"), c("BO"))
    ts(c("NQH"), c("NM"), -2048, None, A.add)
    ts(c("PT"), c("PR"), -1, 15, A.mult, A.add)
    gi(c("KR"), [[0, 24], [-1, 16]], 15, 0, True)
    gi(c("RLi"), [[1, 24]], 0, 0)
    gi(c("JI"), [[16, 8]], 0, 0)
    for x4 in range(2):
        gs((T.PX[:, x4, :], ("PX", x4 * 64, x4 * 64 + 64)), c("ONE", 0, 64), [[-32, 4], [-1, 16]], A.is_equal, -16 * x4, 1)
    for t in range(1, N):
        send(T.cores[(rank + t) % N], T.cores[(rank - t) % N], "l%d" % t, T.LL[:, t, :, :], L3("LL", 0), ("LL", t * 256, t * 256 + 256))
    sset = lambda t: 0 if t % N == 0 else 1 + t % 2
    ms(c("KC", 0, 1), 1.0)
    late[0] = True
    Ib, IND = c("II", 0, 128), c("BOb", 0, 128, 16)

    def statics(t):
        if t == 3:
            yield ("need", ("state", 1, 1))
        if t:
            yield ("need", ("sel", t - 1, 0))
        yield ("need", "col")
        s, ll = sset(t), L3("LL", t % N)
        yield act(L3("OO", s), ll, F.Identity, bias=col(5), scale=16.0)
        yield act(L3("A1", s), ll, F.Copy, bias=352.0)
        yield act(L3("B1", s), ll, F.Copy, bias=1184.0)
        for j, (w, k) in enumerate(((3232, 352), (2400, 1184))):
            yield act((T.SXY[:, s, :, j, :], ("SXY", s * 512, s * 512 + 512)), ll, F.Copy, bias=float(w * k - 2 ** 23 - 13024 * 32), scale=float(w))
        yield ("done", ("statics", t))

    def rows_out():
        for k in range(16):
            b = 512 * (k % 4)
            yield ts(c("SEL", k * 128, k * 128 + 128), c("BOh"), c("DD", k, k + 1), None, A.mult)
            if k > 3:
                yield ("need", ("kept", k - 4))
            yield mm(c("SB", b, b + 256), c("SEL", k * 128, k * 128 + 128), c("NQH"), True, True)
            yield ("done", ("row", k))

    def some_masks():
        for k in range(1, 16, 2):
            a = c("MA", 256 * (k // 2 % 2), 256 * (k // 2 % 2) + 256)
            yield ts(c("KC", k, k + 1), u0, 0, k - 15, A.mult, A.add)
            yield act(a, c("PT"), F.Abs, bias=c("KC", k, k + 1))
            yield act(c("MB", 256 * (k // 2), 256 * (k // 2) + 256), a, F.Relu, bias=c("KC", 0, 1), scale=-1.0)
            yield ("done", ("mask", k))

    def names():
        yield cp(c("Ih"), c("If"))
        for k in range(16):
            b = 512 * (k % 4)
            r = c("PRD", 256 * (k % 2), 256 * (k % 2) + 256)
            if k % 2:
                m = c("MB", 256 * (k // 2), 256 * (k // 2) + 256)
                yield ("need", ("mask", k))
            else:
                m = c("MSK", 256 * (k // 2 % 2), 256 * (k // 2 % 2) + 256)
                yield ts(m, c("PT"), 15 - k, None, A.is_equal)
            yield ("need", ("row", k))
            if k:
                yield last
            yield tt(r, m, c("SB", b, b + 256), A.mult)
            yield ("done", ("kept", k))
            last = mm(c("ST", 0, 256), c("Ih"), r, k == 0, k == 15)
        yield last
        yield cp(c("LPi"), c("ST", 0, 256))
        yield ("done", "names")

    def consts():
        yield ts(col(0), u0, 1, 0, A.mult, A.add)
        yield ts(col(1), u0, -1, 15, A.mult, A.add)
        yield ts(col(5), u0, -1, 15 - 32768, A.mult, A.add)
        yield ("done", "col")
        yield ts(c("FMG"), c("PT"), col(1), None, A.is_equal)
        for q in range(2):
            yield act(c("II", q * 128, q * 128 + 128), c("If"), F.Copy)
        yield ts(col(3), u0, -1, 16, A.mult, A.add)
        yield ts(col(4), u0, 1, 1, A.mult, A.add)
        for q in range(2):
            yield act(c("KDF", q * 128, q * 128 + 128), c("If"), F.Copy, scale=col(3 + q))
        yield ms(c("D0"), 0.0)
        yield ms(c("D0", 0, 256, 16), -1e9)
        yield cp(c("RL"), c("RLi"))
        yield act(c("BOb"), c("BO"), F.Copy)
        yield ms(c("CM"), -128.0)
        yield ms(c("M3"), 0)
        yield ms(c("NC"), 0.0)
        yield ms(c("AT"), 0.0)
        yield ms((T.PM[:, :, :, :, :], ("PM", 0, 512)), 0.0)
        for i in range(4):
            yield cp((T.PM[:, i, :, i % 2, :], ("PM", i * 128, i * 128 + 128)), (T.PX[:, i // 2, :], ("PX", 64 * (i // 2), 64 * (i // 2) + 64)))
        yield act(c("nI"), c("If"), F.Copy, scale=-1.0)
        yield ms(c("COL", 15, 16), 128.0)
        yield ("done", "consts")
        yield cp(c("X", 2048, 2112), c("X", 0, 64))
        yield ("done", ("table", -1, 0))
        yield ("done", ("table", -1, 1))
        yield ("need", ("H", 0, 0))
        for h in range(2):
            yield cp(c("PK", h * 512 + 384, h * 512 + 512), half("PT", h))
        yield act(c("PN"), c("If"), F.Copy, scale=-2.0 ** 25)
        yield ts(c("RX", 0, 8), IND, -512, None, A.mult)
        yield ts(c("RX", 8, 16), IND, 512, None, A.mult)
        yield ts(col(2), u0, -16, 240, A.mult, A.add)
        for q in range(2):
            yield act(c("KD", q * 128, q * 128 + 128), c("If"), F.Copy, scale=col(2))
            yield ms(c("C2", q * 128, q * 128 + 128), (2.0 ** 20, 256.0)[q])
        yield ms(c("OB"), 1.0)
        yield ms(c("O5"), 512.0)
        yield ts(c("COL", 8, 13), c("TH"), -1, -1, A.mult, A.add)
        for t in range(TS):
            yield ts(c("THD", t * 128, t * 128 + 128), c("Ih"), col(8 + t), None, A.mult)
        yield ("done", ("scan", -1, 1))
        yield ts(c("PI2", 2, 4), c("PI", 0, 2), 7, None, A.bitwise_and)
        yield cp(c("RM"), c("PI2", 2, 4))
        yield act(c("M8"), c("DD"), F.Copy, scale=-8.0)
        yield act(c("M1"), c("DD"), F.Copy)
        yield ts(c("JC"), c("JI"), col(0), None, A.add)
        yield ts(c("J8"), c("JC"), 8, None, A.mult)
        yield ("done", "rest")

    def masks(rows, P, i):
        return tt(c(P, i * 512, i * 512 + 384), ind(rows, c("RL")), c("KR"), A.is_equal)

    def new_f(h, s, P, i):
        yield mm(c("ST", 128, 256), c(P, i * 512 + 128, i * 512 + 256), Ib, True, True)
        yield tt(c("MaL"), c("ST", 128, 256), Lh("LL", s[0], h), A.mult)
        yield [mm(c("ST", 384, 512), c("BO"), c("MaL"), True, False), mm(c("ST", 384, 512), c("BOb"), c("CM"), False, True)]
        yield tt(c("ST", 128, 256), c("ST", 384, 512), Lh("B1", s[1], h), A.mult)

    def names_to_H(h, s, H, i):
        yield tt(c("ST", 0, 128), Lh("A1", s[1], h), half("LPi", h), A.mult)
        q = s[1] * 512 + h * 256
        yield tt(c("QQ"), c("ST", 0, 256), (T.SXY[:, s[1], h, :, :], ("SXY", s[1] * 512, s[1] * 512 + 512)), A.add)
        yield ts(c("HB"), c("QQ"), 65535, 5, A.bitwise_and, A.logical_shift_right)
        yield cp(c("HF"), c("HB"))
        yield op("v", lambda e: e.transpose(T[H][:, i, :, :], T.HF[:, :]), (None, (H, i * 256, i * 256 + 256)), c("HF"), dur=190.0)

    def first_state(h):
        if h:
            yield ("need", ("state", -1, 0))
        else:
            for k in ("consts", "names", ("statics", 0)):
                yield ("need", k)
        yield mm(c("ST", 0, 256), half("FMG", h), c("KDF"), True, True)
        sc, r = h * 256, h * 160
        yield ts(c("T1", 0, 128), half("LPi", h), 16, None, A.mult)
        yield tt(c("RI", r, r + 128), c("T1", 0, 128), half("PT", h), A.add)
        yield scan(c("SC", sc, sc + 256), c("ST", 0, 256))
        yield ts(c("M3", h * 24 + 8, h * 24 + 16), c("SC", sc + 15, sc + 128, 16), -1, None, A.add)
        yield ts(c("M3", h * 24 + 16, h * 24 + 24), c("SC", sc + 143, sc + 256, 16), -1, 16, A.mult, A.add)
        yield masks(c("M3", h * 24, h * 24 + 24), "PK", h)
        for x in new_f(h, (0, 0), "PK", h):
            yield x
        for x in names_to_H(h, (0, 0), "HL", h):
            yield x
        yield ("done", ("H", 0, h))
        for e in (128, 152):
            yield cp(c("RI", r + e, r + e + 8), c("M3", h * 24 + 16, h * 24 + 24))
        for k in ("p", "r", "z"):
            yield ("done", (k, 0, h))
        yield ("done", ("state", -1, h))

    def lists(t, h):
        i = t * 2 + h
        yield ("need", ("H", t, h))
        yield ("need", ("scan", t - 1, 1))
        if h:
            yield ("need", ("L", t, 0))
        for ib in range(4):
            p = []
            for x4 in range(2):
                for g2 in range(2):
                    w = ib * 32 + g2 * 16
                    p.append(mm((T.HR[:, :, 2 * ib + x4:128:8], ("HR", 0, 1)), (T.PM[:, 2 * x4 + g2], ("PM", 0, 512)),
                                (T.HL[:, i, :, w:w + 16], ("HL", i * 256, i * 256 + 256)), g2 == 0, g2 == 1))
            yield p
        yield ("need", ("nc", t))
        if h == 0:
            yield ("need", ("g", t - 1, 0))
        yield ts(c("OFF", h * 256, h * 256 + 256), (T.HR[:, :, :], ("HR", 0, 1)), c("NC", t, t + 1), None, A.add)
        yield ("done", ("L", t, h))

    XW = c("X", 0, 2112)

    def raw(h, j):
        return c("WW", h * 4096 + 512 * j, h * 4096 + 512 * j + 512) if j < 4 else c("XR", h * 2048 + 512 * (j - 4), h * 2048 + 512 * (j - 4) + 512)

    def gathers(t, h):
        yield ("need", ("L", t, h))
        yield ("need", ("table", t - 1, 0))
        yield ("need", ("table", t - 1, 1))
        if h:
            yield ("need", ("g", t, 0))
        for j in range(8):
            o = h * 256 + (128 + 32 * j if j < 4 else 32 * (j - 4))
            w = ind(XW, c("OFF", o, o + 32))
            a = act(raw(h, j), w, F.Copy, bias=-128.0 if j < 4 else 0.0)
            if j < 4:
                yield a
            else:
                yield ("alt", a, cp(raw(h, j), w))
            yield ("done", ("g", t, h, j))
        yield ("done", ("g", t, h))

    def minus_z(t, h):
        i = t * 2 + h
        yield ("need", ("z", t, h))
        for j in range(8):
            b, J = 512 * (j % 4), i * 8 + j - 4
            yield ("need", ("g", t, h, j))
            if J >= 0:
                yield ("need", ("abs", J))
            yield [mm(c("SB", b, b + 512), Ib, raw(h, j), True, False)] + \
                [mm(c("SB", b + 128 * r, b + 128 * r + 128), c("nI"), c("ZL", i * 128, i * 128 + 128), False, r == 3) for r in range(4)]
            yield ("done", ("d", t, h, j))

    def absval(t, h):
        for j in range(8):
            yield ("need", ("d", t, h, j))
            b, w = 512 * (j % 4), h * 4096 + 2048 + 512 * (j - 4)
            if j < 4:
                yield act(c("AY", h * 2048 + 512 * j, h * 2048 + 512 * j + 512), c("SB", b, b + 512), F.Abs, bias=c("COL", 15, 16))
            else:
                yield act(c("WW", w, w + 512), c("SB", b, b + 512), F.Abs)
            yield ("done", ("abs", (t * 2 + h) * 8 + j))

    def sums(t, h):
        i = (t * 2 + h) * 512
        yield ("need", ("scan", t - 1 + h, 1 - h))
        yield ("need", ("p", t, h))
        kp = c("KP", 0, 256)
        yield [mm(kp, Ib, c("C2"), True, False), mm(kp, c("OB"), c("KD"), False, False),
               mm(c("KP", 128, 256), c("O5"), c("THD", t * 128, t * 128 + 128), False, False)]
        yield [mm(kp, c("PK", i + 384, i + 512), c("II"), False, False)] + \
            [mm(c("KP", q * 128, q * 128 + 128), c("PN"), c("PK", i + j, i + j + 128), False, False) for q in range(2) for j in (128, 256)]
        for j in range(8):
            yield ("need", ("abs", (t * 2 + h) * 8 + j))
            p = []
            for k in range(4 * (j % 4), 4 * (j % 4) + 4):
                if j < 4:
                    p.append(mm(c("KP", 128 + k, 256, 16), c("AY", h * 2048 + k * 128, h * 2048 + k * 128 + 128), c("RX", 0, 8), False, False))
                else:
                    w = h * 4096 + 2048 + k * 128
                    p.append(mm(c("KP", k, 256, 16), c("WW", w, w + 128), c("RX"), False, k == 15))
            yield p
        yield ("done", ("sums", t, h))

    def choose(t, h):
        sc, e, i = h * 256, (t * 2 + h) * 32, t * 2 + h
        yield ("need", ("sums", t, h))
        yield scan(c("SC", sc, sc + 256), c("KP", 0, 256))
        yield ("done", ("scan", t, h))
        yield ("need", "rest")
        mS, mD = c("SC", sc + 143, sc + 256, 16), c("SC", sc + 15, sc + 128, 16)
        m, a, sel = c("TM", h * 16, h * 16 + 8), c("TM", 32 + h * 16, 40 + h * 16), c("SE", h * 8, h * 8 + 8)
        yield ts(m, mS, 0, 2 ** 21, A.is_ge, A.mult)
        yield tt(a, m, mS, A.add)
        yield tt(sel, a, mD, A.max)
        yield ts(half("KQ", h, 8), sel, 0x1F0, None, A.bitwise_and)
        yield tt(half("GMx", h), ind(half("KQ", h, 8), c("RL", 0, 8)), c("M8"), A.mult)
        yield [mm(c("TL", 0, 8), Ib, c("JC"), True, False), mm(c("TL", 0, 8), half("GMx", h), IND, False, True)]
        yield ts(c("ES", e, e + 32), ind(sel, c("RM")), 2 ** 21, None, A.is_lt)
        yield ("done", ("sel", t, h))
        yield ts(half("LS", h, 8), c("TL", 0, 8), 3968, None, A.add)
        yield act(half("AW", h), ind(half("WW", h, 4096), half("LS", h, 8)), F.Abs)
        z, zn = c("ZL", i * 128, i * 128 + 128), c("ZN", i * 128, i * 128 + 128)
        yield tt(half("SZ", h), ind(half("WW", h, 4096), half("LS", h, 8)), z, A.add)
        yield ts(half("HZ", h), half("SZ", h), 0.5, 63.75, A.mult, A.add)
        yield tt(zn, half("HZ", h), half("AW", h), A.min)
        if t + 1 < TS:
            n = (i + 2) * 128
            yield send(nxt, prv, "az%d%d" % (t + 1, h), T.ZL[:, n:n + 128], zn, ("ZL", n, n + 128))
            yield ("done", ("z", t + 1, h))
        yield mm(c("TL", 8, 16), zn, IND, True, True)
        yield cp(c("UI", h * 16, h * 16 + 8), c("TL", 8, 16))
        yield ts(c("UI", h * 16 + 8, h * 16 + 16), c("UI", h * 16, h * 16 + 8), 7, None, A.bitwise_and)
        yield tt(half("GMx", 2 + h), ind(c("UI", h * 16 + 8, h * 16 + 16), c("RL", 0, 8)), c("M1"), A.mult)
        yield [mm(c("TL", 16, 24), Ib, c("J8"), True, False), mm(c("TL", 16, 24), half("GMx", 2 + h), IND, False, True)]
        yield cp(half("LC", h, 8), c("TL", 16, 24))
        xw = c("X", 1024 * h, 1024 * h + 1024)
        yield tt(half("SX2", h), ind(xw, half("LC", h, 8)), zn, A.add)
        yield ts(half("HX2", h), half("SX2", h), 0.5, -0.25, A.mult, A.add)
        yield ("need", ("g", t, 1))
        yield cp(ind(xw, half("LC", h, 8)), half("HX2", h))
        if h == 0 and t + 1 < TS:
            yield cp(c("X", 2048, 2112), c("X", 0, 64))
        yield ("done", ("table", t, h))

    def count(t):
        yield ("need", ("sel", t, 0))
        yield ("need", ("sel", t, 1))
        yield [mm(c("TL", 24, 32), c("OB"), c("ES", j * 32, j * 32 + 8), j == 0, j == 2 * t + 1) for j in range(2 * t + 2)]
        yield tt(c("DF", 96, 104), c("TL", 24, 32), c("BO", 0, 128, 16), A.mult)
        yield op("v", lambda e: e.tensor_reduce(T.AT[:, t + 1:t + 2], T.DF[:, 96:104], AxisListType.X, A.add), c("AT", t + 1, t + 2), c("DF", 96, 104), dur=130.0)
        if t + 1 < TS:
            yield ts(c("AI", t, t + 1), c("AT", t + 1, t + 2), 1 / 64, -63 / 128, A.mult, A.add)
            yield ts(c("NC", t + 1, t + 2), c("AI", t, t + 1), -64, c("AT", t + 1, t + 2), A.mult, A.add)
            yield ("done", ("nc", t + 1))
        else:
            yield tt(c("YE"), c("AT", 1, 6), c("AT", 0, 5), A.subtract)
            yield out(T.ye[:, :], c("YE"))

    def state(t, h):
        i, s, d = t * 2 + h, (t % N, sset(t)), 48 * h
        sel, e, b, j = c("SE", h * 8, h * 8 + 8), i * 32, i * 160 + 128, i * 512
        yield ("need", ("sel", t, h))
        yield ("need", ("r", t, h))
        yield ts(c("RI", b + 8, b + 16), sel, 4, 15, A.logical_shift_right, A.bitwise_and)
        yield ts(c("RI", b + 16, b + 24), sel, 15, None, A.bitwise_and)
        yield tt(c("DF", d, d + 24), c("RI", b, b + 24), c("RI", b + 8, b + 32), A.subtract)
        yield tt(c("DF", d + 24, d + 48), c("DF", d, d + 24), c("ES", e, e + 24), A.mult)
        yield tt(c("RS", b + 8, b + 32), c("RI", b + 8, b + 32), c("DF", d + 24, d + 48), A.add)
        yield masks(c("RS", b + 8, b + 32), "PS", i)
        yield ("need", ("statics", t % N))
        Qo, Qn, R = c("RI", i * 160, i * 160 + 128), c("RS", i * 160, i * 160 + 128), half("QI2", h)
        yield tt(R, Qo, Lh("OO", s[1], h), A.add)
        yield ("need", ("state", t - 1 + h, 1 - h))
        yield [mm(c("ST", 0, 128), c("PS", j, j + 128), Ib, True, False), mm(c("ST", 0, 128), c("PK", j + 128, j + 256), Ib, False, True)]
        yield tt(c("UO"), c("ST", 0, 128), Lh("OO", s[1], h), A.mult)
        yield mm(c("ST", 256, 384), c("BO"), c("UO"), True, True)
        if t + 1 < TS:
            for x in new_f(h, s, "PS", i):
                yield x
        yield tt(c("R1"), c("ST", 256, 384), R, A.subtract)
        yield tt(c("ST", 256, 384), c("ST", 0, 128), c("R1"), A.mult)
        yield tt(Qn, c("ST", 256, 384), Qo, A.add)
        if t + 1 == TS:
            yield ts(half("Pi", h), Qn, 15, None, A.bitwise_and)
            yield ("done", ("state", t, h))
            return
        yield ts(half("LPi", h), Qn, 4, None, A.arith_shift_right)
        for x in names_to_H(h, s, "HN", i):
            yield x
        n = i + 2

        def ship(k, outap, inap, reg, lreg):
            return send(nxt, prv, "a%s%d%d" % (k, t + 1, h), outap, (inap, reg), lreg)
        yield ship("h", T.HL[:, n, :, :], T.HN[:, i, :, :], ("HN", i * 256, i * 256 + 256), ("HL", n * 256, n * 256 + 256))
        yield ("done", ("H", t + 1, h))
        yield ts(half("Pi", h), Qn, 15, None, A.bitwise_and)
        yield cp(c("PS", j + 384, j + 512), half("Pi", h))
        yield ship("p", T.PK[:, n * 512 + 128:n * 512 + 512], T.PS[:, j + 128:j + 512], ("PS", j + 128, j + 512), ("PK", n * 512 + 128, n * 512 + 512))
        yield ("done", ("p", t + 1, h))
        yield cp(c("RS", b, b + 8), c("RS", b + 24, b + 32))
        yield ship("r", T.RI[:, n * 160:n * 160 + 160], T.RS[:, i * 160:i * 160 + 160], ("RS", i * 160, i * 160 + 160), ("RI", n * 160, n * 160 + 160))
        yield ("done", ("r", t + 1, h))
        yield ("done", ("state", t, h))

    def out(dst, src, q="sy"):
        return give((q, lambda e: e.dma_start(dst, src[0]), [src[1]], [], "out", 16, 60.0, 2200.0, None))

    def finish(h):
        i = 2 * (TS - 1) + h
        j = i * 512
        yield ("need", ("state", TS - 1, h))
        if h:
            yield ("need", ("finish", 0))
        yield cp(half("FA", h, 8), c("RS", i * 160 + 144, i * 160 + 152))
        o = (T.ST[0:8, 384:512], ("ST", 0, 1))
        yield [mm(c("ST", 128, 256), c("PS", j + 128, j + 256), Ib, True, False), mm(c("ST", 128, 256), c("PS", j + 256, j + 384), Ib, False, True),
               mm(o, half("FA", h, 8), Ib, True, True)]
        p = c("P2", 128 * h, 128 * h + 128)
        yield ts(p, half("Pi", h), -1, col(1), A.mult, A.add)
        yield tt(c("T1", 128 * h, 128 * h + 128), c("ST", 128, 256), p, A.mult)
        y = (T.YF[0:8, h * 128:h * 128 + 128], ("YF", h * 128, h * 128 + 128))
        yield ts(y, o, -1, 15, A.mult, A.add)
        yield ("done", ("finish", h))
        yield out(T.yf[:, h * 128:h * 128 + 128], y)
        yield tt(p, c("T1", 128 * h, 128 * h + 128), half("Pi", h), A.add)
        yield ts(half("YP", h), p, -1, 15, A.mult, A.add)
        yield out(T.yp[:, h * 128:h * 128 + 128], half("YP", h))

    def last():
        yield ("need", ("table", TS - 1, 0))
        yield ("need", ("table", TS - 1, 1))
        yield out(T.yx[:, :], c("X", 0, 2048))
        yield out(T.yz[:, :], c("ZN", 8 * 128, 10 * 128), "s")

    th = [(0, some_masks()), (0, rows_out()), (0, names()), (2, consts()), (3, first_state(0)), (4, first_state(1)), (0, last())]
    for t in range(TS):
        for h in range(2):
            th += [(0, lists(t, h)), (0, choose(t, h)), (3 - h, state(t, h)), (5, gathers(t, h)), (4, minus_z(t, h)), (4, absval(t, h)), (4, sums(t, h))]
        th.append((1, count(t)))
        if t < N:
            th.append((6, statics(t)))
    for h in range(2):
        th.append((3, finish(h)))
    ev, live, blocked = {("nc", 0), ("g", -1, 0)}, [], {}

    def pull(rec):
        for x in rec[1]:
            if isinstance(x, tuple) and x[0] == "done":
                ev.add(x[1])
                for r in blocked.pop(x[1], ()):
                    pull(r)
            elif isinstance(x, tuple) and x[0] == "need":
                if x[1] not in ev:
                    blocked.setdefault(x[1], []).append(rec)
                    return
            else:
                rec[2] = x
                live.append(rec)
                return

    def when(x):
        if isinstance(x, list):
            return start(x[0]), x
        if x[0] == "alt":
            a, v = start(x[1]), start(x[2])
            return (v, [x[2]]) if v + x[2][6] + VPEN < a + x[1][6] else (a, [x[1]])
        return start(x), [x]

    for n, (p, gen) in enumerate(th):
        pull([p * 1000 + n, gen, None])
    while live:
        best = None
        for rec in live:
            s, calls = when(rec[2])
            if best is None or (s, rec[0]) < (best[0], best[1][0]):
                best = (s, rec, calls)
        live.remove(best[1])
        for d in best[2]:
            do(d)
        pull(best[1])
    for s in cnt:
        g.wait_ge(sem[s], cnt[s])
    for t in range(1, N):
        g.wait_ge(sem["l%d" % t], len(topo.engines(T.cores[(rank - t) % N], core)[:8]))
    for t in range(1, TS):
        for h in range(2):
            for k in KINDS:
                g.wait_ge(sem["a%s%d%d" % (k, t, h)], len(topo.engines(prv, core)[:8]))
    g.wait_ge(sem.sent, sent[0])
